import numpy as np, ml_dtypes
CORES = [16,17,18,19,32,33,34,35]
N = 8
import mx_ref
BF = ml_dtypes.bfloat16
def cut(t, i, w=512):
    return t[:, w * i:w * i + w]
def tile(rs):
    return np.stack(rs, axis=2).reshape(128, -1).astype(BF)
def pick(q, e):
    c = np.concatenate([q[0].reshape(128, -1, 4), np.zeros((128, 1, 4), np.uint8)], axis=1); s = np.concatenate([q[1], np.ones((16, 1), np.uint8)], axis=1)
    return (np.ascontiguousarray(c[:, e].reshape(128, -1)), np.ascontiguousarray(s[:, e]))
def join(*qs):
    return (np.concatenate([q[0] for q in qs], axis=1), np.concatenate([q[1] for q in qs], axis=1))
def put(q, e, v):
    c, s = q[0].reshape(128, -1, 4).copy(), q[1].copy(); c[:, e] = v[0].reshape(128, -1, 4); s[:, e] = v[1]
    return (c.reshape(128, -1), s)
def pk(c, s):
    return (np.ascontiguousarray(c), mx_ref.live(s))
def emit(q):
    return q[0], q[1]
def f(rng, *shape):
    return mx_ref.flush((rng.standard_normal(shape, dtype=np.float32) * np.exp2(rng.integers(-2, 3, shape[:-1] + (1,)))).astype(BF))
def wide(rng, *shape, cols=0):
    v = rng.standard_normal(shape, dtype=np.float32) * np.exp2(rng.integers(-12, 13, shape)).astype(np.float32)
    if cols: v *= np.repeat(np.exp2(rng.integers(-cols, cols + 1, shape[:-2] + (1, shape[-1] // 4))) * (rng.random(shape[:-2] + (1, shape[-1] // 4)) > 0.0625), 4, axis=-1).astype(np.float32)
    return mx_ref.flush(v.astype(BF))
T, G, CS, R = 64, 128, 16, 4
def game(x, qx, w, u):
    wq = [[mx_ref.quantize(np.ascontiguousarray(cut(w[r], i))) for i in range(4)] for r in range(N)]
    uq = [mx_ref.quantize(np.ascontiguousarray(u[r])) for r in range(N)]
    wait = join(*[mx_ref.quantize(np.ascontiguousarray(qx[m])) for m in range(N)])
    s = [mx_ref.quantize(np.ascontiguousarray(x[r])) for r in range(N)]
    num = [r * T + np.arange(T) for r in range(N)]
    log, said, made, head = [[] for r in range(N)], [[] for r in range(N)], [], 0
    for t in range(R):
        for r in range(N):
            a = tile([np.maximum(mx_ref.matmul(wq[r][i], s[r]), np.float32(0)) * np.float32(0.0625) for i in range(4)])
            made.append(a)
            s[r] = mx_ref.quantize(a)
            h = mx_ref.matmul(uq[r], s[r])[:2] + np.float32(0)
            stop = np.flatnonzero(h[0] > h[1])[:CS]
            if stop.size == 0: continue
            log[r].append(pick(s[r], stop))
            said[r].extend(num[r][stop].tolist())
            g = head + np.arange(stop.size)
            s[r] = put(s[r], stop, pick(wait, G * (g % N) + g // N))
            num[r][stop] = N * T + g
            head += stop.size
    return log, said, s, num, made
def fit(d, top=2.0 ** 30):
    try:
        with np.errstate(all="ignore"):
            a = np.abs(np.stack(game(d["x"], d["qx"], d["w"], d["u"])[4]).astype(np.float32))
    except Exception: return False
    return bool(np.isfinite(a).all() and ((a == 0) | (a >= 2.0 ** -30) & (a <= top)).all())
def first(make, top=2.0 ** 30):
    for i in range(5):
        d = make()
        if fit(d, top): break
    return d
def plain(rng):
    w = np.rint(rng.standard_normal((N, 128, 2048), dtype=np.float32) * 8) * 0.125 * np.exp2(rng.integers(-1, 2, (N, 128, 1))) + 0.0
    u = np.zeros((N, 128, 512), np.float32)
    u[:, :, :8] = rng.standard_normal((N, 128, 8))
    u[:, :, 4:8] += 0.15 * rng.random((N, 1, 1))
    u *= np.exp2(rng.integers(-1, 2, (N, 128, 1)))
    return {"x": np.array(f(rng, N, 128, 4 * T)), "qx": np.array(f(rng, N, 128, 4 * G)), "w": w.astype(BF), "u": np.array(mx_ref.flush(u.astype(BF))), "v": np.array(f(rng, N, 128, 512))}
def channel(w, alone=False):
    a = w.astype(np.float32).reshape(N, 128, 4, 128, 4)
    if alone: a[:, :8] = 0
    a[:, :, :, :8, :] = 0
    for i in range(4):
        for j in range(8): a[:, j, i, j, i] = 16
    return a.reshape(N, 128, 2048).astype(BF)
def flags(d, live, wait):
    d["x"][:, :8] = np.repeat(np.where(live, 4.0, 0.0), 4, axis=1)[:, None, :].astype(BF)
    d["qx"][:, :8] = np.repeat(np.where(wait.reshape(G, N).T, 4.0, 0.0), 4, axis=1)[:, None, :].astype(BF)
def signed(t, a, b):
    o = np.abs(t.astype(np.float32))
    o[:, :4] *= a
    o[:, 4:8] *= b
    return o.astype(BF)
def setup_inputs(rng):
    return first(lambda: plain(rng), 2.0 ** 8)
def setup_inputs_many(rng):
    def make():
        d = plain(rng)
        d["w"] = channel(d["w"])
        pair = rng.integers(0, 2, N * G // 2)
        flags(d, np.stack([rng.permutation(T) < 3 * T // 4 for r in range(N)]), np.stack([pair, 1 - pair], axis=1).reshape(-1) == 1)
        for r in range(N):
            a = np.zeros((128, 512), np.float32)
            a[:8, :4] = 1
            a[8:, 4:8] = np.abs(rng.standard_normal((120, 4))) * 2.0 ** -8
            d["u"][r] = mx_ref.flush(a.astype(BF))
        return d
    return first(make)
def setup_inputs_none(rng):
    def make():
        d = plain(rng)
        a, b = rng.permutation(N)[:2]
        d["u"][a] = signed(d["u"][a], -1, 1)
        d["u"][b] = signed(d["u"][b], 1, -1)
        return d
    return first(make)
def setup_inputs_ties(rng):
    def make():
        d = plain(rng)
        d["w"] = channel(d["w"])
        flags(d, np.stack([rng.permutation(T) < T // 3 for r in range(N)]), rng.random(N * G) < 0.3)
        d["u"][:, :, 4:8] = d["u"][:, :, :4]
        d["u"][:, :8, :4] = 1
        d["u"][:, :8, 4:8] = 0
        a, c = rng.permutation(N)[:2]
        d["u"][a, :, 4:8] = d["u"][a, :, :4]
        d["u"][c] = 0
        d["u"][c, :7, :8] = 1
        d["u"][c, 7, :4] = 2.0 ** -8
        d["u"][c, 7, 4:8] = 2.0 ** -9
        return d
    return first(make)
def setup_inputs_zero(rng):
    def make():
        d = plain(rng)
        d["w"] = channel(d["w"], alone=True)
        live = np.stack([rng.permutation(np.repeat([0, 1, 2], [T - 2 * (T // 8), T // 8, T // 8])) for r in range(N)])
        for k, e in (("x", live), ("qx", rng.choice(3, (N, G), p=[0.75, 0.125, 0.125]))):
            m = np.repeat(e, 4, axis=1)[:, None, :]
            c = np.where(m == 0, d[k].astype(np.float32), np.float32(0))
            c[:, :8] = np.where(m == 2, np.float32(-4), c[:, :8])
            d[k] = c.astype(BF)
        for r in rng.permutation(N)[:N // 2]: d["u"][r] = signed(d["u"][r], 1, -1)
        return d
    return first(make)
def setup_inputs_spread(rng):
    return first(lambda: {**plain(rng), "x": wide(rng, N, 128, 4 * T, cols=6), "qx": wide(rng, N, 128, 4 * G, cols=6)})
def check_inputs(d):
    b = []
    for k in ("x", "qx", "w", "u", "v"):
        a = np.abs(d[k].astype(np.float32))
        if not (np.isfinite(a).all() and ((a == 0) | (a >= 2.0 ** -30) & (a <= 2.0 ** 30)).all()): b.append("a value of " + k)
    if (d["u"][:, :, 8:].astype(np.float32) != 0).any(): b.append("u has numbers behind its first two columns")
    if not b and not fit(d): b.append("a number that a layer makes")
    return b
def reference(x, qx, w, u, v):
    log, said, s, num, made = game(x, qx, w, u)
    M = R * CS + T
    oc, osc = np.zeros((N, 128, 4 * M), np.uint8), np.zeros((N, 16, M), np.uint8)
    sid, y = np.full((N, 1, M), -1, np.float32), np.zeros((N, 128, T), np.float32)
    for r in range(N):
        n = len(said[r])
        oc[r], osc[r] = emit(pick(join(*log[r], s[r]), np.concatenate([np.arange(n), np.full(R * CS - n, -1), n + np.arange(T)])))
        sid[r, 0, :n] = said[r]
        sid[r, 0, R * CS:] = num[r]
        y[r] = mx_ref.matmul(mx_ref.quantize(np.ascontiguousarray(v[r])), s[r])
    return {"oc": oc, "osc": osc, "sid": sid, "y": y}

@@ -1,0 +1,764 @@
+from concourse.bass import DstId, RemoteDMATransfer
+from concourse.mybir import dt, AluOpType, AxisListType, ActivationFunctionType
+
+OP = AluOpType
+ACT = ActivationFunctionType
+X4 = "float8_e4m3fn_x4"
+NR, PL, CS, RD = 8, 64, 16, 4
+PICKS = {
+    "s1": (1, 7, "win", [{4: (1, 4, 0), 5: (1, 4, 2), 6: (1, 4, 4), 7: (1, 4, 6), 0: (2, 4, 8), 1: (2, 4, 8)}]),
+    "s2": (2, 3, "mid", [{2: (2, 4, 4), 3: (2, 4, 6), 4: (2, 4, 8), 5: (2, 4, 8)}, {6: (2, 8, 8), 7: (2, 8, 8)}]),
+    "s3": (3, 1, "low", [{0: (3, 4, 0), 1: (3, 4, 2), 2: (3, 4, 4), 3: (3, 4, 4)}, {4: (3, 8, 4), 5: (3, 8, 4)}]),
+    "s4": (3, 6, "two", [{6: (3, 2, 12), 7: (3, 2, 14)}]),
+    "s5": (4, 5, "end", [dict([(q, (4, 2, 2 * q)) for q in range(7)]), {7: (4, 4, 12)}]),
+}
+ADV = dict([(q, (1, 8, 64)) for q in range(4)])
+RECV = {}
+for _q in ADV:
+    RECV[1, _q] = (8, -1, ADV)
+for _n in PICKS:
+    for _c in PICKS[_n][3]:
+        for _q in _c:
+            RECV[_c[_q][0], _q] = (_c[_q][1], -1 if _c[_q][0] > PICKS[_n][0] else PICKS[_n][1], _c)
+ALL = list(range(NR))
+TELL = {1: [("ca1", ALL, ALL)], 2: [("ca2", [0, 1, 2, 3], ALL), ("cb2", [4, 5, 6, 7], ALL)],
+        3: [("ca3", [0, 1], ALL), ("cb3", [2, 3, 4], ALL), ("cc3", [5, 6], ALL), ("cd3", [7], ALL)],
+        4: [("ca4", [0, 1, 2, 3, 4, 5], ALL), ("cb4", [6], [7])]}
+LOAD = {"dx": 2.2, "dq": 1.9, "du": 2.0, "dw0": 2.7, "dw1": 3.2, "dw2": 3.7, "dw3": 4.2}
+EST = {"wake": 0.12, "look": 0.04, "part": 0.3, "hold": 0.2, "issue": 0.12, "transfer": 0.03, "first": 1.0, "fly": 0.8, "rows": 0.115,
+       "near": 0.3, "far": 0.5, "on": 1.5, "off": 1.7, "dma": 1.8}
+ORDER = {}
+
+SCRATCH = {
+    "f": ("sbuf", [128, 6000], "float32"),
+    "cnt": ("sbuf", [128, 264], "bfloat16"),
+    "iw": ("sbuf", [128, 768], "int32"),
+    "ow": ("sbuf", [128, 256], "uint16"),
+    "xt": ("sbuf", [128, 512], "bfloat16"),
+    "wt": ("sbuf", [128, 2048], "bfloat16"),
+    "us": ("sbuf", [128, 8], "bfloat16"),
+    "ut": ("sbuf", [128, 512], "bfloat16"),
+    "vt": ("sbuf", [128, 512], "bfloat16"),
+    "zt": ("sbuf", [128, 512], "bfloat16"),
+    "pl": ("psum", [128, 2048], "float32"),
+    "pd0": ("psum", [128, 512], "float32"),
+    "pd1": ("psum", [128, 512], "float32"),
+    "py": ("psum", [128, 512], "float32"),
+}
+
+
+def _pair(name, n):
+    SCRATCH[name + "c"] = ("sbuf", [128, n], X4)
+    SCRATCH[name + "p"] = ("sbuf", [128, n], "uint8")
+
+
+for _n in ("ta1", "tl1", "tl2"):
+    SCRATCH[_n] = ("sbuf", [128, 512], "bfloat16")
+for _k in range(1, RD + 1):
+    SCRATCH["cu%d" % _k] = ("sbuf", [128, 72], "bfloat16")
+    SCRATCH["cs%d" % _k] = ("sbuf", [128, 96], "bfloat16")
+for _n, _w in (("zq", 128), ("xq", 128), ("wq", 512), ("uq", 128), ("u2", 256), ("vq", 128), ("m0", 128), ("m1", 192), ("m2", 192),
+               ("m3", 192), ("a2", 128), ("a3", 128), ("ff", 128), ("l1", 128), ("l2", 128), ("l3", 128), ("lg", 128), ("fin", 128)):
+    _pair(_n, _w)
+for _n in PICKS:
+    _pair(_n, 16)
+
+SEMAPHORES = ["qv", "qs", "qt", "qg", "sent", "dx", "dw0", "dw1", "dw2", "dw3", "du", "dq", "dv", "p1", "p2", "p3", "p4", "p5", "pg",
+              "oc1", "oc2", "oy", "osid", "osc"]
+SEMAPHORES += ["%s%d" % (_n, _k) for _n in ("own", "col") for _k in range(1, RD + 1)]
+SEMAPHORES += [_g[0] for _k in range(1, RD + 1) for _g in TELL[_k]]
+
+
+def _pow2(n):
+    k = 1
+    while 2 * k <= n:
+        k *= 2
+    return k
+
+
+def _share(cores, pool):
+    k = _pow2(len(pool) // len(cores)) if cores else 0
+    return {d: pool[i * k:i * k + k] for i, d in enumerate(cores)}
+
+
+def _engine_sets(topo, cores, s, who, wide=0):
+    me = cores[s]
+    away = [c for c in cores if topo.chip(c) != topo.chip(me)]
+    pool = topo.engines(me, away[0])
+    dst = [cores[q] for q in who if q != s]
+    far = [d for d in dst if d in away]
+    out = _share(far, pool if len(far) > 1 else pool[-(len(pool) // len(away)):])
+    home = [d for d in dst if d not in away]
+    if wide and home and not far:
+        every = topo.engines(me, home[0])
+        return _share(home, every if wide == 1 else every[::-1])
+    if home:
+        out.update(_share(home, [e for e in topo.engines(me, home[0]) if e not in pool]))
+    return out
+
+
+def build(g, T, topo, r):
+    cores = T.cores
+    core = cores[r]
+    Q = {"v": g.vector, "s": g.scalar, "t": g.tensor, "g": g, "y": g.sync}
+    nodes, log, total, late = [], {}, {}, []
+
+    def node(q, calls, reads, writes, dur, sem=None, to=None):
+        deps, ext = set(), {}
+        for lst, wr in ((reads, False), (writes, True)):
+            for (n, a, b) in lst:
+                for (c, d, w, who) in log.get(n, []):
+                    if a < d and c < b and (w or wr):
+                        if isinstance(who, int):
+                            deps.add(who)
+                        else:
+                            ext[who[0]] = who[1]
+        i = len(nodes)
+        nodes.append({"q": q, "calls": calls, "deps": deps, "ext": ext, "dur": dur, "sem": sem, "to": to or []})
+        for n, a, b in reads:
+            log[n] = log.get(n, []) + [(a, b, False, i)]
+        for n, a, b in writes:
+            log[n] = [e for e in log.get(n, []) if not (a <= e[0] and e[1] <= b)] + [(a, b, True, i)]
+        return i
+
+    def dma(q, sem, items):
+        total[sem] = 16 * len(items)
+        ids = []
+        for o, i, rd, wr in items:
+            ids.append(node(q, [lambda o=o, i=i: Q[q].dma_start(o, i)], rd, wr, 0.06, sem))
+        for k in ids:
+            nodes[k]["batch"] = ids
+        return ids
+
+    def rf(n, a, b, st=1):
+        return (n, a, b, st)
+
+    def ap(x):
+        n, a, b, st = x
+        return T[n][:, a:b] if st == 1 else T[n][:, a:b:st]
+
+    def rg(*xs):
+        return [(x[0], x[1], x[2]) for x in xs if isinstance(x, tuple)]
+
+    def sv(x):
+        return ap(x) if isinstance(x, tuple) else x
+
+    def cols(x):
+        return len(range(x[1], x[2], x[3]))
+
+    pos = {"f": 0, "iw": 0, "ow": 0}
+
+    def new(buf, n, al=8):
+        a = -(-pos[buf] // al) * al
+        pos[buf] = a + n
+        return rf(buf, a, a + n)
+
+    def fl(n):
+        return new("f", n)
+
+    def sub(x, a, b, st=1):
+        return rf(x[0], x[1] + a, x[1] + b, st)
+
+    def vt(n):
+        return 0.04 + 0.001 * max(64, n)
+
+    def it(n):
+        return 0.06 + 0.0015 * n
+
+    def ts(out, i, s1, s2, o0, o1=None):
+        if o1 is None:
+            f = lambda: g.vector.tensor_scalar(ap(out), ap(i), sv(s1), None, o0)
+        else:
+            f = lambda: g.vector.tensor_scalar(ap(out), ap(i), sv(s1), sv(s2), o0, o1)
+        node("v", [f], rg(i, s1, s2), rg(out), vt(cols(i)))
+
+    def tt(out, a, b, o):
+        node("v", [lambda: g.vector.tensor_tensor(ap(out), ap(a), ap(b), o)], rg(a, b), rg(out), vt(2 * cols(a)))
+
+    def cp(out, i):
+        node("v", [lambda: g.vector.tensor_copy(ap(out), ap(i))], rg(i), rg(out), vt(cols(i)))
+
+    def scan(out, d0, d1, init, o0, o1):
+        return node("v", [lambda: g.vector.tensor_tensor_scan(ap(out), ap(d0), ap(d1), sv(init), o0, o1)], rg(d0, d1, init), rg(out),
+                    vt(cols(d0)))
+
+    def fill(x, val, tag=None):
+        node("v", [lambda: g.vector.memset(ap(x), val)], [], [tag] if tag else rg(x), vt(cols(x) // 2))
+
+    def act(out, i, func, scale=1.0, bias=0.0, acc=None):
+        kw = {}
+        if acc is not None:
+            kw["accum_out"] = ap(acc)
+        if scale != 1.0:
+            kw["scale"] = sv(scale)
+        if bias != 0.0:
+            kw["bias"] = sv(bias)
+        node("s", [lambda: g.scalar.activation(ap(out), ap(i), func, **kw)], rg(i, scale, bias), rg(out) + (rg(acc) if acc else []), vt(cols(i)))
+
+    def gather(out, win, off):
+        node("s", [lambda: g.scalar.activation(ap(out), ap(win).indirect(ap(off)), ACT.Copy)], rg(win, off), rg(out), it(cols(out)))
+
+    def total_of(out, i):
+        act(fl(cols(i)), i, ACT.Copy, acc=out)
+
+    def pick(dst, a, b, src, c, d, off):
+        dc, dp, sc, sp = dst + "c", dst + "p", src + "c", src + "p"
+        node("v", [lambda: g.vector.tensor_copy(T[dc][:, a:b].bitcast(dt.uint32), T[sc][:, c:d].bitcast(dt.uint32).indirect(ap(off)))],
+             [(sc, c, d)] + rg(off), [(dc, a, b)], it(b - a))
+        node("s", [lambda: g.scalar.activation(T[dp][:, a:b], T[sp][:, c:d].indirect(ap(off)), ACT.Copy)],
+             [(sp, c, d)] + rg(off), [(dp, a, b)], it(b - a))
+
+    def quant(dst, a, b, tile, c, d, regs):
+        node("v", [lambda: g.vector.quantize_mx(T[dst + "c"][:, a:b], T[dst + "p"][:, a:b], T[tile][:, c:d])], regs,
+             [(dst + "c", a, b), (dst + "p", a, b)], 0.15)
+
+    def mm(out, bank, st, a, mv, c, start, stop):
+        return lambda: g.tensor.matmul_mx(T[out][:, 512 * bank:512 * bank + 128], T[st + "c"][:, a:a + 128], T[st + "p"][:, a:a + 128],
+                                          T[mv + "c"][:, c:c + 128], T[mv + "p"][:, c:c + 128], start, stop)
+
+    def mmr(st, a, mv, c):
+        return [(st + "c", a, a + 128), (st + "p", a, a + 128), (mv + "c", c, c + 128), (mv + "p", c, c + 128)]
+
+    def layer(mv, c, tile, n, dst, a, vec):
+        for b in range(4):
+            node("t", [mm("pl", b, "wq", 128 * b, mv, c, True, True)], mmr("wq", 128 * b, mv, c), [("pl", 512 * b, 512 * b + 512)], 0.17)
+
+        def relu(b):
+            src, out = T.pl[:, 512 * b:512 * b + n], T[tile][:, b:4 * n:4]
+            w = [("%s.%d" % (tile, b), 0, 1)]
+            rd = [("pl", 512 * b, 512 * b + 512)]
+            if b in vec:
+                node("v", [lambda: g.vector.tensor_scalar(out, src, 0.0, 0.0625, OP.max, OP.mult)], rd, w, vt(n))
+            else:
+                node("s", [lambda: g.scalar.activation(out, src, ACT.Relu, scale=0.0625)], rd, w, vt(n))
+        for b in range(4):
+            relu(b)
+        quant(dst, a, a + 128, tile, 0, 512, [("%s.%d" % (tile, b), 0, 1) for b in range(4)] + [(tile + ".z", 0, 1)])
+
+    def diff(pd, mv, c):
+        node("t", [mm(pd, 0, "u2", 0, mv, c, True, False), mm(pd, 0, "u2", 128, mv, c, False, True)],
+             mmr("u2", 0, mv, c) + mmr("u2", 128, mv, c), [(pd, 0, 512)], 0.34)
+
+    land = {1: ("l1", 0), 2: ("l2", 0), 3: ("l3", 0), 4: ("ff", 64)}
+
+    def send(who, sem, src, dst, regs, wide=0):
+        dsts = [q for q in who if q != r]
+        if not dsts:
+            return
+        eng = _engine_sets(topo, cores, r, dsts, wide)
+        tr = []
+        for q in dsts:
+            rid, pid, _s = topo.addr(cores[q])
+            m = 0
+            for e in eng[cores[q]]:
+                m |= 1 << e
+            tr.append(RemoteDMATransfer(dst_ids=[DstId(rid=rid, pnc=pid)], dma_engine_mask=m, remote_sem=T.sem[sem(q)], src=src(q), dst=dst(q)))
+            total["sent"] = total.get("sent", 0) + len(eng[cores[q]])
+        node("g", [lambda: g.remote_dma_fused(tr, local_sem=T.sem.sent)], regs, [], EST["issue"] + EST["transfer"] * len(tr), "sent",
+             [(q, sem(q)) for q in dsts])
+
+    def send_pair(call, name):
+        def view(q, x):
+            t, W, _a = call[q]
+            nm, c0 = land[t]
+            return T[nm + x][:, c0 + W * r:c0 + W * r + W]
+
+        def mine(q, x):
+            _t, W, a = call[q]
+            return T[name + x][:, a:a + W]
+        sem = lambda q: "col%d" % call[q][0]
+        for x in "cp":
+            reg = [(name + x, call[q][2], call[q][2] + call[q][1]) for q in call if q != r]
+            if x == "c":
+                send(call, sem, lambda q: mine(q, "c").bitcast(dt.uint8), lambda q: view(q, "c").bitcast(dt.uint8), reg, 1 if call is ADV else 0)
+            else:
+                send(call, sem, lambda q: mine(q, "p"), lambda q: view(q, "p"), reg, 2 if call is ADV else 0)
+
+    def own(call, name):
+        if r not in call:
+            return
+        t, W, b = call[r]
+        nm, c0 = land[t]
+        a = c0 + W * r
+        dma("y", "own%d" % t, [(T[nm + "c"][:, a:a + W].bitcast(dt.uint8), T[name + "c"][:, b:b + W].bitcast(dt.uint8),
+                                [(name + "c", b, b + W)], [(nm + "c", a, a + W)]),
+                               (T[nm + "p"][:, a:a + W], T[name + "p"][:, b:b + W], [(name + "p", b, b + W)], [(nm + "p", a, a + W)])])
+
+    def engines_in(s, who):
+        return len(_engine_sets(topo, cores, s, who, 1 if who is ADV else 0)[core])
+
+    def cc(t, s):
+        return 8 * NR * (RD - t) + 8 * (NR - 1 - s)
+
+    width, known = {}, {}
+    for t in range(1, RD + 1):
+        W, top, call = RECV[t, r]
+        width[t], known[t] = W, min(top, r - 1)
+        total["col%d" % t] = sum(2 * engines_in(s, call) for s in ALL if s != r)
+        nm, c0 = land[t]
+        for s in ALL:
+            if s != r:
+                for x in "cp":
+                    log[nm + x] = log.get(nm + x, []) + [(c0 + W * s, c0 + W * s + W, True, ("col%d" % t, total["col%d" % t]))]
+        for nm, grp, to in TELL[t]:
+            grp = [s for s in grp if s != r and r in to]
+            if grp:
+                total[nm] = sum(engines_in(s, to) for s in grp)
+            for s in grp:
+                log["cnt"] = log.get("cnt", []) + [(cc(t, s), cc(t, s) + 1, True, (nm, total[nm]))]
+    nl = {t: NR * width[t] for t in width}
+    exact = {t: known[t] == r - 1 for t in known}
+    ahead = RECV[1, r][2] is ADV
+
+    dma("y", "dx", [(T.xt[:, 0:256], T.x[:, :], [], [("xt", 0, 256)])])
+    dma("s", "dq", [(T.xt[:, 256:512], T.qx[:, 0:256], [], [("xt", 256, 512)])])
+    dma("y", "dw0", [(T.wt[:, 0:512], T.w[:, 0:512], [], [("wt", 0, 512)])])
+    dma("s", "du", [(T.us[:, 0:8], T.u[:, 0:8], [], [("us", 0, 8)])])
+    dma("s", "dw1", [(T.wt[:, 512:1024], T.w[:, 512:1024], [], [("wt", 512, 1024)])])
+    dma("y", "dw2", [(T.wt[:, 1024:1536], T.w[:, 1024:1536], [], [("wt", 1024, 1536)])])
+    dma("s", "dw3", [(T.wt[:, 1536:2048], T.w[:, 1536:2048], [], [("wt", 1536, 2048)])])
+
+    fill(rf("zt", 0, 512), 0.0)
+    quant("zq", 0, 128, "zt", 0, 512, [("zt", 0, 512)])
+
+    def pad(sem, nm, a):
+        if a < 128:
+            return dma("y", sem, [(T[nm + "c"][:, a:128].bitcast(dt.uint8), T.zqc[:, a:128].bitcast(dt.uint8), [("zqc", a, 128)],
+                                   [(nm + "c", a, 128)]),
+                                  (T[nm + "p"][:, a:128], T.zqp[:, a:128], [("zqp", a, 128)], [(nm + "p", a, 128)])])
+        return []
+    fill(rf("ut", 8, 512), 0.0)
+    lu = new("ow", 16, 2)
+    fill(sub(lu, 0, 8), 0)
+    fill(sub(lu, 8, 16), 1)
+    fill(rf("ta1", 256, 512), 0.0, ("ta1.z", 0, 1))
+    six = fl(96)
+    fill(six, 16.0)
+    quant("xq", 0, 128, "xt", 0, 512, [("xt", 0, 512)])
+    send_pair(ADV, "xq")
+    act(rf("ut", 0, 4), rf("us", 0, 4), ACT.Copy)
+    act(rf("ut", 4, 8), rf("us", 4, 8), ACT.Copy, scale=-1.0)
+    quant("uq", 0, 128, "ut", 0, 512, [("ut", 0, 512)])
+    pick("u2", 0, 256, "uq", 0, 128, lu)
+    for b in range(4):
+        quant("wq", 128 * b, 128 * b + 128, "wt", 512 * b, 512 * b + 512, [("wt", 512 * b, 512 * b + 512)])
+    CU = {t: rf("cu%d" % t, 8, 72) for t in range(1, RD + 1)}
+    CN = {t: rf("cu%d" % t, 71, 72) for t in range(1, RD + 1)}
+    fill(rf("cnt", 8 * NR * RD, 8 * NR * RD + 8), 0.0)
+    for t in range(1, RD + 1):
+        fill(rf("cu%d" % t, 0, 8), 0.0)
+    own(ADV, "xq")
+    pad("p1", "l1", nl[1])
+
+    def iota(out, pattern, base, ch):
+        n = 1
+        for _st, c in pattern:
+            n *= c
+        if out[0] == "iw":
+            f = lambda: g.iota(ap(out), pattern, base, ch)
+        else:
+            f = lambda: g.iota(ap(out), pattern, base, ch, allow_small_or_imprecise_dtypes=True)
+        node("g", [f], [], rg(out), 0.13 + 0.0017 * n)
+
+    NC = NR * RD + 1
+    ip, i33 = new("iw", 1), fl(NC)
+    iota(ip, [[0, 1]], 0, 1)
+    iota(i33, [[1, NC]], 0, 0)
+    pl16, q4, nx = fl(64), fl(4), fl(64)
+    iota(pl16, [[0, 4], [1, 16]], 0, 0)
+    iota(q4, [[16, 4]], 0, 0)
+    iota(nx, [[1, 64]], PL * r - NR * PL, 0)
+    if ahead:
+        dstat = fl(nl[1])
+        iota(dstat, [[1, 8], [8, width[1]]], 0, 0)
+    tabs = {}
+    for t in range(1, RD + 1):
+        W = width[t]
+        if W not in tabs and not (t == 1 and ahead):
+            tabs[W] = (fl(8 * W), fl(8 * W), fl(8 * W), fl(8 * W))
+            iota(tabs[W][0], [[-1, 8], [8, W]], 0, 0)
+            iota(tabs[W][1], [[1, 8], [0, W]], 0, 0)
+    NW = {t: fl(64 + nl[t]) for t in range(1, RD + 1)}
+    WW = {t: fl(64 + nl[t]) for t in range(1, RD)}
+    jf, t8, t8w, k0, jh = fl(1), fl(1), fl(1), fl(1), fl(1)
+    i1, i2, i3 = new("iw", 1), new("iw", 1), new("iw", 1)
+    big, wm, rst, p4, hm, hw = fl(1), fl(64), fl(64), fl(4), fl(NC), fl(9)
+    ts(i1, ip, 15, None, OP.bitwise_and)
+    ts(i2, i1, 1, None, OP.logical_shift_right)
+    ts(i3, i1, 1, None, OP.bitwise_and)
+    fill(big, 1e29)
+    ts(t8w, i2, -1.0, 4.0, OP.mult, OP.add)
+    ts(k0, i3, 8.0, 3.5 - r, OP.mult, OP.add)
+    KT = {"two": k0}
+
+    def table(names, first):
+        a, b, c = fl(1), fl(1), fl(1)
+        ts(a, i2, float(first), 0.0, OP.subtract, OP.max)
+        ts(b, a, 16.0, None, OP.mult)
+        tt(c, k0, b, OP.add)
+        for n in names:
+            KT[n] = c
+    table(("win", "mid"), 4)
+    ts(t8w, t8w, 0.0, None, OP.max)
+    ts(big, big, 1e9, None, OP.mult)
+    ts(jf, i1, 0.0, None, OP.add)
+    ts(hw, sub(i33, 0, 9), t8w, None, OP.not_equal)
+    ts(t8, i2, -1.0, 8.0, OP.mult, OP.add)
+    ts(wm, pl16, jf, None, OP.is_equal)
+    ts(rst, pl16, 0.5, None, OP.is_gt)
+    ts(hm, i33, t8, None, OP.not_equal)
+    ts(p4, q4, jf, None, OP.add)
+    ts(jh, jf, 0.5, None, OP.add)
+    table(("end",), 6)
+    table(("low",), 2)
+    act(sub(NW[1], 0, 64), nx, ACT.Copy, scale=0.125)
+    if ahead:
+        act(sub(NW[1], 64, 64 + nl[1]), dstat, ACT.Copy, scale=0.125)
+    for W in tabs:
+        ts(tabs[W][2], tabs[W][0], 3.5, None, OP.add)
+        act(tabs[W][3], tabs[W][1], ACT.Copy, scale=0.125)
+    LN = fl(128)
+    if nl[1] < 128:
+        fill(rf("tl1", 4 * nl[1], 512), 0.0, ("tl1.z", 0, 1))
+    fill(rf("tl2", 4 * nl[2], 512), 0.0, ("tl2.z", 0, 1))
+    fill(sub(LN, 64, 128), -64.125)
+    late += pad("p2", "l2", nl[2])
+    late += pad("p4", "a2", 64)
+    late += dma("y", "dv", [(T.vt[:, :], T.v[:, :], [], [("vt", 0, 512)])])
+    late += pad("p3", "l3", nl[3])
+    late += pad("p5", "a3", 64)
+    late += dma("y", "pg", [(T.lgc[:, 64:128].bitcast(dt.uint8), T.zqc[:, 64:128].bitcast(dt.uint8), [("zqc", 64, 128)], [("lgc", 64, 128)]),
+                            (T.lgp[:, 64:128], T.zqp[:, 64:128], [("zqp", 64, 128)], [("lgp", 64, 128)])])
+    BR, FB, NOLD, THR, LIST, KK, STW, STS, SLOT, CF, stop, LC = {}, {}, {}, {}, {}, {}, {}, {}, {}, {}, {}, {}
+    acc = [p4]
+    place = {1: "m0", 2: "a2", 3: "a3", 4: "ff"}
+    WP = {t: fl(64) for t in range(1, RD + 1)}
+
+    def tell(t, src):
+        me = rf("cnt", cc(t, r), cc(t, r) + 1)
+        for nm, grp, to in TELL[t]:
+            if r in grp:
+                send(to, lambda q: nm, lambda q: ap(src), lambda q: ap(me), rg(src))
+        act(me, src, ACT.Copy)
+
+    def stops(t):
+        k = scan(CU[t], WP[t], sub(six, 0, 64), 0.0, OP.add, OP.min)
+        if t == 1:
+            for i in late:
+                nodes[i]["deps"].add(k)
+            tell(1, CN[1])
+        stop[t] = fl(64)
+        tt(stop[t], CU[t], rf("cu%d" % t, 7, 71), OP.subtract)
+        CF[t] = fl(1)
+        act(CF[t], CN[t], ACT.Copy)
+
+    def old(t):
+        to = fl(64)
+        act(to, stop[t], ACT.Copy, scale=big)
+        layer(place[t], 0, "ta1", 64, "m%d" % t, 0, (0,))
+        diff("pd0", "m%d" % t, 0)
+        w, NOLD[t] = sub(WW[t], 0, 64), fl(1)
+        tt(w, rf("pd0", 0, 64), to, OP.is_gt)
+        total_of(NOLD[t], w)
+
+    def wrap(t):
+        k, a, b = fl(64), fl(64), fl(64)
+        tt(k, stop[t], CU[t], OP.mult)
+        tt(a, k, wm, OP.mult)
+        scan(b, rst, a, 0.0, OP.mult, OP.add)
+        KK[t], STW[t] = sub(b, 15, 64, 16), fl(4)
+        act(STW[t], KK[t], ACT.Sign)
+        e, f, STS[t] = fl(4), fl(4), fl(4)
+        act(STS[t], STW[t], ACT.Copy, scale=float(width[t]))
+        act(e, STW[t], ACT.Copy, scale=64.0)
+        if exact[t]:
+            h = fl(4)
+            ts(f, KK[t], 8.5, None, OP.is_ge)
+            tt(h, e, f, OP.add)
+            e = h
+        SLOT[t] = fl(4)
+        tt(SLOT[t], e, p4, OP.max)
+
+    def since(t, first):
+        return rf("cnt", cc(t, first), 8 * NR * RD, 8)
+
+    def base(t):
+        BR[t] = fl(1)
+        if r == 0 and t == 1:
+            fill(BR[t], 0.0)
+        elif r == 0:
+            total_of(BR[t], since(t - 1, NR - 1))
+        else:
+            total_of(BR[t], since(t, r - 1))
+
+    def window(t):
+        if t == 1 and ahead:
+            return
+        if exact[t]:
+            FB[t] = BR[t]
+        else:
+            FB[t] = fl(1)
+            total_of(FB[t], since(t, known[t]) if known[t] >= 0 else since(t - 1, NR - 1))
+        n, W = nl[t], width[t]
+        i = new("iw", n)
+        ts(i, tabs[W][2], FB[t], 0.125, OP.add, OP.mult)
+        tt(sub(NW[t], 64, 64 + n), i, tabs[W][3], OP.add)
+
+    def threshold(t):
+        n8, e, f, hi = sub(NW[t], 64, 64 + nl[t]), fl(1), fl(1), fl(nl[t])
+        act(f, BR[t], ACT.Copy, scale=0.125)
+        act(e, CF[t], ACT.Identity, scale=0.125, bias=f)
+        ts(hi, n8, e, big, OP.is_ge, OP.mult)
+        THR[t] = hi
+        if not exact[t]:
+            lo, THR[t] = fl(nl[t]), fl(nl[t])
+            ts(lo, n8, f, big, OP.is_lt, OP.mult)
+            tt(THR[t], lo, hi, OP.max)
+
+    def make_list(t):
+        LIST[t] = new("ow", 4, 2)
+        gi, mi = new("iw", 4), new("iw", 4)
+        ts(gi, KK[t], BR[t], -1.0, OP.add, OP.add)
+        ts(mi, gi, 7, None, OP.bitwise_and)
+        a, b = fl(4), fl(4)
+        tt(a, mi, STS[t], OP.mult)
+        slot = SLOT[t]
+        if not exact[t]:
+            di, si, w, slot = gi, new("iw", 4), fl(4), fl(4)
+            if t in FB:
+                d, di = fl(4), new("iw", 4)
+                ts(d, KK[t], FB[t], -1.0, OP.subtract, OP.add)
+                ts(di, d, BR[t], None, OP.add)
+            ts(si, di, 3, None, OP.arith_shift_right)
+            tt(w, si, STW[t], OP.mult)
+            tt(slot, w, SLOT[t], OP.add)
+        tt(b, a, slot, OP.add)
+        cp(LIST[t], b)
+
+    def merge(t):
+        e = 64 + nl[t]
+        gather(WP[t + 1], sub(WW[t], 0, e), LIST[t])
+        pick(place[t + 1], 0, 64, "m%d" % t, 0, e, LIST[t])
+
+    def newcomers(t):
+        layer(land[t][0], land[t][1], "tl1" if t == 1 else "tl2", nl[t], "m%d" % t, 64, (0, 2))
+        diff("pd1", "m%d" % t, 64)
+
+    def count(t):
+        n = nl[t]
+        ww = sub(WW[t], 64, 64 + n)
+        tt(ww, rf("pd1", 0, n), THR[t], OP.is_gt)
+        if any(r in grp for _nm, grp, _to in TELL[t + 1]):
+            cs = rf("cs%d" % (t + 1), 0, n)
+            scan(cs, ww, sub(six, 0, n), NOLD[t], OP.add, OP.min)
+            tell(t + 1, rf(cs[0], n - 1, n))
+
+    def source(name):
+        t, top, tab, calls = PICKS[name]
+        a = NR - 1 - top
+        n = NR * t + 1 - a
+        s, o = fl(n), new("ow", 1, 2)
+        m = hw if tab == "win" else hm
+        scan(s, sub(m, a, a + n), rf("cnt", cc(t, top), 8 * NR * RD + 1, 8), 0.0, OP.mult, OP.add)
+        ts(o, sub(s, n - 1, n), KT[tab], 0.125, OP.add, OP.mult)
+        pick(name, 0, 16, "xq", 64, 128, o)
+        for call in calls:
+            send_pair(call, name)
+        for call in calls:
+            own(call, name)
+
+    def take_log(t):
+        a, b = fl(63), fl(1)
+        o = new("ow", 1, 2)
+        act(a, sub(CU[t], 0, 63), ACT.Sign, scale=-1.0, bias=jh, acc=b)
+        ts(o, b, 63.0, 0.5, OP.add, OP.mult)
+        pick("lg", 16 * t - 16, 16 * t, place[t], 0, 64, o)
+        gather(sub(LN, 16 * t - 16, 16 * t), sub(NW[t], 0, 64), o)
+        LC[t] = CF[t]
+        if t > 1:
+            LC[t] = fl(1)
+            act(LC[t], CF[t], ACT.Identity, bias=LC[t - 1])
+        m, c, d = fl(1), fl(4), fl(4)
+        ts(m, CF[t], -1.0, 16.0, OP.mult, OP.add)
+        ts(c, p4, LC[t], m, OP.is_ge, OP.mult)
+        tt(d, acc[-1], c, OP.add)
+        acc.append(d)
+
+    layer("xq", 0, "ta1", 64, "m0", 0, (0, 2))
+    diff("pd0", "m0", 0)
+    ts(WP[1], rf("pd0", 0, 64), 0.0, None, OP.is_gt)
+    stops(1)
+    source("s1")
+    for t in (1, 2, 3):
+        if t > 1:
+            merge(t - 1)
+            stops(t)
+        old(t)
+        if t == 3:
+            source("s4")
+        base(t)
+        window(t)
+        threshold(t)
+        newcomers(t)
+        count(t)
+        if t == 2:
+            source("s3")
+        wrap(t)
+        make_list(t)
+        if t == 1:
+            source("s2")
+        else:
+            gather(sub(NW[t], 0, 64), NW[t - 1], LIST[t - 1])
+    merge(3)
+    stops(4)
+    source("s5")
+    base(4)
+    window(4)
+    wrap(4)
+    make_list(4)
+    gather(sub(NW[4], 0, 64), NW[3], LIST[3])
+
+    for t in (1, 2, 3):
+        take_log(t)
+    quant("vq", 0, 128, "vt", 0, 512, [("vt", 0, 512)])
+    take_log(4)
+    lx = new("ow", 4, 2)
+    cp(lx, acc[-1])
+    pick("fin", 0, 64, "lg", 0, 128, lx)
+    nn, sid, sid2 = fl(128), fl(128), fl(128)
+    gather(sub(nn, 0, 64), LN, lx)
+    gather(sub(nn, 64, 128), NW[4], LIST[4])
+    act(sid, nn, ACT.Copy, scale=8.0)
+    ts(sid2, sid, float(NR * PL), None, OP.add)
+    dma("y", "oc1", [(T.oc[:, 0:256], T.finc[:, 0:64].bitcast(dt.uint8), [("finc", 0, 64)], [])])
+    dma("y", "osid", [(T.sid[:, :], T.f[0:1, sid2[1]:sid2[2]], rg(sid2), [])])
+
+    pick("fin", 64, 128, "ff", 0, 64 + nl[4], LIST[4])
+    dma("y", "oc2", [(T.oc[:, 256:512], T.finc[:, 64:128].bitcast(dt.uint8), [("finc", 64, 128)], [])])
+    node("t", [mm("py", 0, "vq", 0, "fin", 0, True, True)], mmr("vq", 0, "fin", 0), [("py", 0, 512)], 0.17)
+    ys = fl(64)
+    cp(ys, rf("py", 64, 128))
+    dma("y", "oy", [(T.y[:, :], ap(ys), rg(ys), [])])
+    dma("s", "osc", [(T.osc[4 * k:4 * k + 4, :], T.finp[32 * k:32 * k + 4, :], [("finp", 0, 128)], []) for k in range(4)])
+
+    for k, nd in enumerate(nodes):
+        more = set()
+        for d in nd["deps"]:
+            more |= set(nodes[d].get("batch", []))
+        nd["deps"] = (nd["deps"] | more) - {k}
+    return nodes, total, Q
+
+
+def timetable(graphs, cores, topo):
+    N = {(r, k): nd for r, nodes in enumerate(graphs) for k, nd in enumerate(nodes)}
+
+    def away(i, j):
+        return topo.chip(cores[i[0]]) != topo.chip(cores[j[0]])
+    come = {}
+    for i in N:
+        for q, sem in N[i]["to"]:
+            come.setdefault((q, sem), []).append(i)
+    pred, succ = {}, {i: [] for i in N}
+    for i in N:
+        p = [((i[0], d), EST["wake"]) for d in N[i]["deps"]]
+        for sem in N[i]["ext"]:
+            p += [(j, EST["wake"] + (EST["off"] if away(i, j) else EST["on"])) for j in come[i[0], sem]]
+        pred[i] = p
+        for j, w in p:
+            succ[j].append((i, w))
+
+    def length(i):
+        sem = N[i]["sem"]
+        return N[i]["dur"] if sem is None or sem == "sent" else LOAD.get(sem, EST["dma"])
+
+    rest, unmet = {}, {i: len(succ[i]) for i in N}
+    todo = [i for i in N if not unmet[i]]
+    while todo:
+        i = todo.pop()
+        rest[i] = length(i) + max([0.0] + [w + rest[j] for j, w in succ[i]])
+        for j, w in pred[i]:
+            unmet[j] -= 1
+            if not unmet[j]:
+                todo.append(j)
+
+    missing, at = {i: len(pred[i]) for i in N}, {i: 0.0 for i in N}
+    free, ready, lane, land, first = {}, {}, {}, {}, set()
+    order = [[] for _g in graphs]
+
+    def put(i):
+        ready.setdefault((i[0], N[i]["q"]), []).append(i)
+    for i in N:
+        if not missing[i]:
+            put(i)
+    while any(ready.values()):
+        best = None
+        for k in ready:
+            if ready[k]:
+                f = free.get(k, 0.0)
+                cand = [(max(f, at[i]), -1e3 if N[i]["sem"] in LOAD else -rest[i], i) for i in ready[k]]
+                c = min(cand)
+                lim = c[0] + (EST["hold"] if k[1] == "g" else EST["look"] + EST["part"] * N[c[2]]["dur"])
+                c = min((c for c in cand if c[0] <= lim), key=lambda c: (c[1], c[2]))
+                if best is None or lim < best[0]:
+                    best = (lim, c)
+        s, _p, i = best[1]
+        nd = N[i]
+        k = (i[0], nd["q"])
+        ready[k].remove(i)
+        order[i[0]].append(i[1])
+        d = nd["dur"]
+        if nd["sem"] == "sent" and i[0] not in first:
+            first.add(i[0])
+            d += EST["first"]
+        free[k] = s + d
+        fin = s + (d if nd["sem"] == "sent" else length(i))
+        for far in (True, False):
+            n = len([q for q, _s in nd["to"] if away(i, (q, 0)) == far])
+            if n:
+                land[far] = lane[i[0], far] = max(fin + EST["fly"], lane.get((i[0], far), 0.0)) + EST["rows"] * n
+        for j, w in succ[i]:
+            f = fin + w
+            if j[0] != i[0]:
+                far = away(i, j)
+                f = land[far] + EST["wake"] + (EST["far"] if far else EST["near"])
+            at[j] = max(at[j], f)
+            missing[j] -= 1
+            if not missing[j]:
+                put(j)
+    return order
+
+
+def rank_program(g, core, T, topo):
+    r = T.rank_of(core)
+    if r is None:
+        return
+    if not ORDER:
+        for q, o in enumerate(timetable([build(g, T, topo, q)[0] for q in ALL], T.cores, topo)):
+            ORDER[q] = o
+    nodes, total, Q = build(g, T, topo, r)
+    value, seen = {}, {q: {} for q in Q}
+    for k in ORDER[r]:
+        nd = nodes[k]
+        q, sem = nd["q"], nd["sem"]
+        want = dict(nd["ext"])
+        for d in nd["deps"]:
+            want[value[d][0]] = max(want.get(value[d][0], 0), value[d][1])
+        for w in want:
+            if seen[q].get(w, 0) < want[w]:
+                Q[q].wait_ge(T.sem[w], want[w])
+                seen[q][w] = want[w]
+        for c in nd["calls"][:-1]:
+            c()
+        if sem is None:
+            total["q" + q] = total.get("q" + q, 0) + 1
+            nd["calls"][-1]().then_inc(T.sem["q" + q], 1)
+            value[k] = ("q" + q, total["q" + q])
+        elif sem == "sent":
+            nd["calls"][-1]()
+            value[k] = ("sent", 0)
+        else:
+            nd["calls"][-1]().then_inc(T.sem[sem], 16)
+            value[k] = (sem, total[sem])
+    for sem in total:
+        if seen["g"].get(sem, 0) < total[sem]:
+            g.wait_ge(T.sem[sem], total[sem])

@@ -5,44 +5,46 @@ OP = AluOpType
 ACT = ActivationFunctionType
 X4 = "float8_e4m3fn_x4"
 NR, PL, CS, RD = 8, 64, 16, 4
-PICKS = {
-    "s1": (1, 7, "win", [{4: (1, 4, 0), 5: (1, 4, 2), 6: (1, 4, 4), 7: (1, 4, 6), 0: (2, 4, 8), 1: (2, 4, 8)}]),
-    "s2": (2, 3, "mid", [{2: (2, 4, 4), 3: (2, 4, 6), 4: (2, 4, 8), 5: (2, 4, 8)}, {6: (2, 8, 8), 7: (2, 8, 8)}]),
-    "s3": (3, 1, "low", [{0: (3, 4, 0), 1: (3, 4, 2), 2: (3, 4, 4), 3: (3, 4, 4)}, {4: (3, 8, 4), 5: (3, 8, 4)}]),
-    "s4": (3, 6, "two", [{6: (3, 2, 12), 7: (3, 2, 14)}]),
-    "s5": (4, 5, "end", [dict([(q, (4, 2, 2 * q)) for q in range(7)]), {7: (4, 4, 12)}]),
-}
-ADV = dict([(q, (1, 8, 64)) for q in range(4)])
-RECV = {}
-for _q in ADV:
-    RECV[1, _q] = (8, -1, ADV)
-for _n in PICKS:
-    for _c in PICKS[_n][3]:
-        for _q in _c:
-            RECV[_c[_q][0], _q] = (_c[_q][1], -1 if _c[_q][0] > PICKS[_n][0] else PICKS[_n][1], _c)
 ALL = list(range(NR))
-TELL = {1: [("ca1", ALL, ALL)], 2: [("ca2", [0, 1, 2, 3], ALL), ("cb2", [4, 5, 6, 7], ALL)],
-        3: [("ca3", [0, 1], ALL), ("cb3", [2, 3, 4], ALL), ("cc3", [5, 6], ALL), ("cd3", [7], ALL)],
-        4: [("ca4", [0, 1, 2, 3, 4, 5], ALL), ("cb4", [6], [7])]}
-LOAD = {"dx": 2.2, "dq": 1.9, "du": 2.0, "dw0": 2.7, "dw1": 3.2, "dw2": 3.7, "dw3": 4.2}
-EST = {"wake": 0.12, "look": 0.04, "part": 0.3, "hold": 0.2, "issue": 0.12, "transfer": 0.03, "first": 1.0, "fly": 0.8, "rows": 0.115,
-       "near": 0.3, "far": 0.5, "on": 1.5, "off": 1.7, "dma": 1.8}
+NS = 31
+TELL = {}
+for _r in ALL:
+    TELL[1, _r] = ("t1", ALL, _r, [])
+    TELL[2, _r] = ("e1", list(range(_r + 1, 4)), 27 + _r, []) if _r < 3 else ("t2", ALL, _r + 5, [27, 28, 29] if _r == 3 else [])
+    TELL[3, _r] = ("t2", ALL, _r + 13, []) if _r < 3 else ("t3", ALL, _r + 12, [30] if _r == 5 else [])
+    TELL[4, _r] = ("t3", ALL, _r + 20, []) if _r < 5 else ("e4", list(range(_r + 1, NR)), _r + 20, [])
+TELL[3, 3] = ("e2", ALL, 16, [])
+TELL[3, 4] = ("e3", [5], 30, [])
+LAND = {}
+for _r in ALL:
+    LAND[1, _r] = ("adv", 8, 0, 0, list(range(_r))) if _r < 3 else ("r1", 2, 2 * _r - 6, _r, [])
+    LAND[2, _r] = ("r2", 2, 2 * _r - 10, _r + 5, [])
+    LAND[3, _r] = ("r2", 2, 2 * _r + 6, _r + 13, [])
+    LAND[4, _r] = ("r3", 2, 2 * _r, _r + 20, [])
+LAND.update({(2, 0): ("r1", 6, 10, 8, []), (2, 1): ("r1", 6, 10, 8, [27]), (2, 2): ("r1", 6, 10, 8, [27, 28]),
+             (2, 3): ("r1b", 10, 6, 8, [27, 28, 29]), (2, 4): ("r1b", 10, 6, 8, [8]),
+             (3, 3): ("r2", 4, 12, 16, []), (3, 4): ("r2", 4, 12, 16, [16]),
+             (3, 5): ("r2b", 8, 8, 16, [16, 30]), (3, 6): ("r2b", 8, 8, 16, [16, 17]), (3, 7): ("r2c", 8, 8, 17, [17, 18]),
+             (4, 5): ("r3", 6, 10, 25, []), (4, 6): ("r3", 6, 10, 25, [25]), (4, 7): ("r3", 6, 10, 25, [25, 26])})
+PICKS = {"r1": (8, 3, 5), "r2": (16, 2, 6), "r3": (25, 3, 5), "r1b": (8, 0, 0), "r2b": (16, 0, 0), "r2c": (17, 0, 0)}
+OFF = 4000.0
+LOAD = {"du": 1.8, "dh": 1.9, "dx": 2.2, "dw0": 2.7, "dw1": 3.2, "dw2": 3.7, "dw3": 4.2, "dq": 4.5}
+EST = {"wake": 0.12, "gap": 0.03, "grain": 0.02, "issue": 0.15, "transfer": 0.03, "first": 1.5, "fly": 0.6, "rows": 1.2, "near": 0.7, "far": 0.8,
+       "hop": 2.0, "dma": 1.8, "loaded": 4.3, "again": 0.5, "most": 0.5, "slow": 1.25}
 ORDER = {}
 
 SCRATCH = {
     "f": ("sbuf", [128, 6000], "float32"),
-    "cnt": ("sbuf", [128, 264], "bfloat16"),
+    "cnt": ("sbuf", [128, 8 * NS], "bfloat16"),
     "iw": ("sbuf", [128, 768], "int32"),
     "ow": ("sbuf", [128, 256], "uint16"),
     "xt": ("sbuf", [128, 512], "bfloat16"),
+    "qt": ("sbuf", [128, 512], "bfloat16"),
     "wt": ("sbuf", [128, 2048], "bfloat16"),
-    "us": ("sbuf", [128, 8], "bfloat16"),
-    "ut": ("sbuf", [128, 512], "bfloat16"),
     "vt": ("sbuf", [128, 512], "bfloat16"),
-    "zt": ("sbuf", [128, 512], "bfloat16"),
+    "tl": ("sbuf", [128, 640], "bfloat16"),
     "pl": ("psum", [128, 2048], "float32"),
-    "pd0": ("psum", [128, 512], "float32"),
-    "pd1": ("psum", [128, 512], "float32"),
+    "pd": ("psum", [128, 512], "float32"),
     "py": ("psum", [128, 512], "float32"),
 }
 
@@ -52,56 +54,57 @@ def _pair(name, n):
     SCRATCH[name + "p"] = ("sbuf", [128, n], "uint8")
 
 
-for _n in ("ta1", "tl1", "tl2"):
-    SCRATCH[_n] = ("sbuf", [128, 512], "bfloat16")
 for _k in range(1, RD + 1):
-    SCRATCH["cu%d" % _k] = ("sbuf", [128, 72], "bfloat16")
-    SCRATCH["cs%d" % _k] = ("sbuf", [128, 96], "bfloat16")
-for _n, _w in (("zq", 128), ("xq", 128), ("wq", 512), ("uq", 128), ("u2", 256), ("vq", 128), ("m0", 128), ("m1", 192), ("m2", 192),
-               ("m3", 192), ("a2", 128), ("a3", 128), ("ff", 128), ("l1", 128), ("l2", 128), ("l3", 128), ("lg", 128), ("fin", 128)):
+    SCRATCH["cs%d" % _k] = ("sbuf", [128, 160], "bfloat16")
+    _pair("a%d" % _k, 224)
+    _pair("m%d" % _k, 160)
+for _n, _w in (("xq", 128), ("qq", 128), ("wq", 512), ("u2", 256), ("vq", 128), ("lg", 128), ("fin", 128), ("r1b", 16), ("r2b", 16), ("r2c", 16)):
     _pair(_n, _w)
-for _n in PICKS:
-    _pair(_n, 16)
 
-SEMAPHORES = ["qv", "qs", "qt", "qg", "sent", "dx", "dw0", "dw1", "dw2", "dw3", "du", "dq", "dv", "p1", "p2", "p3", "p4", "p5", "pg",
-              "oc1", "oc2", "oy", "osid", "osc"]
-SEMAPHORES += ["%s%d" % (_n, _k) for _n in ("own", "col") for _k in range(1, RD + 1)]
-SEMAPHORES += [_g[0] for _k in range(1, RD + 1) for _g in TELL[_k]]
-
-
-def _pow2(n):
-    k = 1
-    while 2 * k <= n:
-        k *= 2
-    return k
+SEMAPHORES = ["qv", "qs", "qt", "qg", "sent", "oc1", "oc2", "oy", "osid", "osc", "dv"] + list(LOAD)
+SEMAPHORES += [_n + _x for _n in ("t1", "t2", "t3", "e1", "e2", "e3", "e4") for _x in "nf"]
+SEMAPHORES += ["col%d" % _k for _k in range(1, RD + 1)]
 
 
 def _share(cores, pool):
-    k = _pow2(len(pool) // len(cores)) if cores else 0
+    k = 1
+    while cores and 2 * k * len(cores) <= len(pool):
+        k *= 2
     return {d: pool[i * k:i * k + k] for i, d in enumerate(cores)}
 
 
-def _engine_sets(topo, cores, s, who, wide=0):
-    me = cores[s]
-    away = [c for c in cores if topo.chip(c) != topo.chip(me)]
-    pool = topo.engines(me, away[0])
-    dst = [cores[q] for q in who if q != s]
-    far = [d for d in dst if d in away]
-    out = _share(far, pool if len(far) > 1 else pool[-(len(pool) // len(away)):])
-    home = [d for d in dst if d not in away]
-    if wide and home and not far:
-        every = topo.engines(me, home[0])
-        return _share(home, every if wide == 1 else every[::-1])
-    if home:
-        out.update(_share(home, [e for e in topo.engines(me, home[0]) if e not in pool]))
-    return out
+def _away(topo, cores, s, q):
+    return topo.chip(cores[s]) != topo.chip(cores[q])
+
+
+def _pools(topo, cores, s):
+    far = topo.engines(cores[s], [cores[q] for q in ALL if _away(topo, cores, s, q)][0])
+    every = topo.engines(cores[s], [cores[q] for q in ALL if q != s and not _away(topo, cores, s, q)][0])
+    return far, [e for e in every if e not in far], every
+
+
+def _engine_sets(topo, cores, s, name, back=False):
+    far, near, every = _pools(topo, cores, s)
+    who = [q for (t, q) in sorted(LAND) if LAND[t, q][0] == name and q != s]
+    out, home = [q for q in who if _away(topo, cores, s, q)], [q for q in who if not _away(topo, cores, s, q)]
+    if name == "adv":
+        near = every
+    if back:
+        far, near = far[::-1], near[::-1]
+    return dict(list(_share(out, far).items()) + list(_share(home, near).items()))
+
+
+def _mask(engines):
+    m = 0
+    for e in engines:
+        m |= 1 << e
+    return m
 
 
 def build(g, T, topo, r):
     cores = T.cores
-    core = cores[r]
     Q = {"v": g.vector, "s": g.scalar, "t": g.tensor, "g": g, "y": g.sync}
-    nodes, log, total, late = [], {}, {}, []
+    nodes, log, total, early = [], {}, {}, []
 
     def node(q, calls, reads, writes, dur, sem=None, to=None):
         deps, ext = set(), {}
@@ -114,7 +117,7 @@ def build(g, T, topo, r):
                         else:
                             ext[who[0]] = who[1]
         i = len(nodes)
-        nodes.append({"q": q, "calls": calls, "deps": deps, "ext": ext, "dur": dur, "sem": sem, "to": to or []})
+        nodes.append({"q": q, "calls": calls, "deps": deps, "ext": ext, "dur": dur * (1.0 if sem else EST["slow"]), "sem": sem, "to": to or []})
         for n, a, b in reads:
             log[n] = log.get(n, []) + [(a, b, False, i)]
         for n, a, b in writes:
@@ -138,7 +141,11 @@ def build(g, T, topo, r):
         return T[n][:, a:b] if st == 1 else T[n][:, a:b:st]
 
     def rg(*xs):
-        return [(x[0], x[1], x[2]) for x in xs if isinstance(x, tuple)]
+        out = []
+        for x in xs:
+            if isinstance(x, tuple):
+                out += [(x[0], x[1], x[2])] if x[3] == 1 else [(x[0], c, c + 1) for c in range(x[1], x[2], x[3])]
+        return out
 
     def sv(x):
         return ap(x) if isinstance(x, tuple) else x
@@ -171,19 +178,23 @@ def build(g, T, topo, r):
         else:
             f = lambda: g.vector.tensor_scalar(ap(out), ap(i), sv(s1), sv(s2), o0, o1)
         node("v", [f], rg(i, s1, s2), rg(out), vt(cols(i)))
+        return out
 
     def tt(out, a, b, o):
-        node("v", [lambda: g.vector.tensor_tensor(ap(out), ap(a), ap(b), o)], rg(a, b), rg(out), vt(2 * cols(a)))
+        node("v", [lambda: g.vector.tensor_tensor(ap(out), ap(a), ap(b), o)], rg(a, b), rg(out), vt((1 if a[0] == "pd" else 2) * cols(a)))
+        return out
 
     def cp(out, i):
         node("v", [lambda: g.vector.tensor_copy(ap(out), ap(i))], rg(i), rg(out), vt(cols(i)))
+        return out
 
     def scan(out, d0, d1, init, o0, o1):
-        return node("v", [lambda: g.vector.tensor_tensor_scan(ap(out), ap(d0), ap(d1), sv(init), o0, o1)], rg(d0, d1, init), rg(out),
-                    vt(cols(d0)))
+        node("v", [lambda: g.vector.tensor_tensor_scan(ap(out), ap(d0), ap(d1), sv(init), o0, o1)], rg(d0, d1, init), rg(out), vt(cols(d0)))
+        return out
 
-    def fill(x, val, tag=None):
-        node("v", [lambda: g.vector.memset(ap(x), val)], [], [tag] if tag else rg(x), vt(cols(x) // 2))
+    def fill(x, val, tags=None):
+        node("v", [lambda: g.vector.memset(ap(x), val)], [], tags or rg(x), vt(cols(x) // (1 if x[0] == "f" else 2)))
+        return x
 
     def act(out, i, func, scale=1.0, bias=0.0, acc=None):
         kw = {}
@@ -194,12 +205,14 @@ def build(g, T, topo, r):
         if bias != 0.0:
             kw["bias"] = sv(bias)
         node("s", [lambda: g.scalar.activation(ap(out), ap(i), func, **kw)], rg(i, scale, bias), rg(out) + (rg(acc) if acc else []), vt(cols(i)))
+        return out
+
+    def line(i, scale, bias):
+        return act(fl(cols(i)), i, ACT.Identity, scale=scale, bias=bias)
 
     def gather(out, win, off):
         node("s", [lambda: g.scalar.activation(ap(out), ap(win).indirect(ap(off)), ACT.Copy)], rg(win, off), rg(out), it(cols(out)))
-
-    def total_of(out, i):
-        act(fl(cols(i)), i, ACT.Copy, acc=out)
+        return out
 
     def pick(dst, a, b, src, c, d, off):
         dc, dp, sc, sp = dst + "c", dst + "p", src + "c", src + "p"
@@ -208,436 +221,334 @@ def build(g, T, topo, r):
         node("s", [lambda: g.scalar.activation(T[dp][:, a:b], T[sp][:, c:d].indirect(ap(off)), ACT.Copy)],
              [(sp, c, d)] + rg(off), [(dp, a, b)], it(b - a))
 
-    def quant(dst, a, b, tile, c, d, regs):
-        node("v", [lambda: g.vector.quantize_mx(T[dst + "c"][:, a:b], T[dst + "p"][:, a:b], T[tile][:, c:d])], regs,
-             [(dst + "c", a, b), (dst + "p", a, b)], 0.15)
+    def quant(dst, n, tile, c, regs, a=0):
+        return node("v", [lambda: g.vector.quantize_mx(T[dst + "c"][:, a:a + n], T[dst + "p"][:, a:a + n], T[tile][:, c:c + 4 * n])], regs,
+                    [(dst + "c", a, a + n), (dst + "p", a, a + n)], 0.04 + 0.001 * n)
 
-    def mm(out, bank, st, a, mv, c, start, stop):
-        return lambda: g.tensor.matmul_mx(T[out][:, 512 * bank:512 * bank + 128], T[st + "c"][:, a:a + 128], T[st + "p"][:, a:a + 128],
-                                          T[mv + "c"][:, c:c + 128], T[mv + "p"][:, c:c + 128], start, stop)
+    def mm(out, bank, st, a, mv, c, n, start, stop):
+        return lambda: g.tensor.matmul_mx(T[out][:, 512 * bank:512 * bank + n], T[st + "c"][:, a:a + 128], T[st + "p"][:, a:a + 128],
+                                          T[mv + "c"][:, c:c + n], T[mv + "p"][:, c:c + n], start, stop)
 
-    def mmr(st, a, mv, c):
-        return [(st + "c", a, a + 128), (st + "p", a, a + 128), (mv + "c", c, c + 128), (mv + "p", c, c + 128)]
+    def mmr(st, a, mv, c, n):
+        return [(st + "c", a, a + 128), (st + "p", a, a + 128), (mv + "c", c, c + n), (mv + "p", c, c + n)]
 
-    def layer(mv, c, tile, n, dst, a, vec):
+    TL = [("tl.%d" % b, 0, 1) for b in range(4)]
+
+    def layer(mv, c, real, at, dst):
+        n = max(128, real)
         for b in range(4):
-            node("t", [mm("pl", b, "wq", 128 * b, mv, c, True, True)], mmr("wq", 128 * b, mv, c), [("pl", 512 * b, 512 * b + 512)], 0.17)
+            node("t", [mm("pl", b, "wq", 128 * b, mv, c, n, True, True)], mmr("wq", 128 * b, mv, c, n), [("pl", 512 * b, 512 * b + 512)],
+                 0.0012 * (n + 16))
 
         def relu(b):
-            src, out = T.pl[:, 512 * b:512 * b + n], T[tile][:, b:4 * n:4]
-            w = [("%s.%d" % (tile, b), 0, 1)]
+            src, out = T.pl[:, 512 * b:512 * b + real], T.tl[:, 4 * at + b:4 * (at + real):4]
             rd = [("pl", 512 * b, 512 * b + 512)]
-            if b in vec:
-                node("v", [lambda: g.vector.tensor_scalar(out, src, 0.0, 0.0625, OP.max, OP.mult)], rd, w, vt(n))
+            if b % 2:
+                node("v", [lambda: g.vector.tensor_scalar(out, src, 0.0, 0.0625, OP.max, OP.mult)], rd, [TL[b]], vt(real))
             else:
-                node("s", [lambda: g.scalar.activation(out, src, ACT.Relu, scale=0.0625)], rd, w, vt(n))
+                node("s", [lambda: g.scalar.activation(out, src, ACT.Relu, scale=0.0625)], rd, [TL[b]], vt(real))
         for b in range(4):
             relu(b)
-        quant(dst, a, a + 128, tile, 0, 512, [("%s.%d" % (tile, b), 0, 1) for b in range(4)] + [(tile + ".z", 0, 1)])
-
-    def diff(pd, mv, c):
-        node("t", [mm(pd, 0, "u2", 0, mv, c, True, False), mm(pd, 0, "u2", 128, mv, c, False, True)],
-             mmr("u2", 0, mv, c) + mmr("u2", 128, mv, c), [(pd, 0, 512)], 0.34)
-
-    land = {1: ("l1", 0), 2: ("l2", 0), 3: ("l3", 0), 4: ("ff", 64)}
-
-    def send(who, sem, src, dst, regs, wide=0):
-        dsts = [q for q in who if q != r]
-        if not dsts:
-            return
-        eng = _engine_sets(topo, cores, r, dsts, wide)
-        tr = []
-        for q in dsts:
-            rid, pid, _s = topo.addr(cores[q])
-            m = 0
-            for e in eng[cores[q]]:
-                m |= 1 << e
-            tr.append(RemoteDMATransfer(dst_ids=[DstId(rid=rid, pnc=pid)], dma_engine_mask=m, remote_sem=T.sem[sem(q)], src=src(q), dst=dst(q)))
-            total["sent"] = total.get("sent", 0) + len(eng[cores[q]])
-        node("g", [lambda: g.remote_dma_fused(tr, local_sem=T.sem.sent)], regs, [], EST["issue"] + EST["transfer"] * len(tr), "sent",
-             [(q, sem(q)) for q in dsts])
-
-    def send_pair(call, name):
-        def view(q, x):
-            t, W, _a = call[q]
-            nm, c0 = land[t]
-            return T[nm + x][:, c0 + W * r:c0 + W * r + W]
-
-        def mine(q, x):
-            _t, W, a = call[q]
-            return T[name + x][:, a:a + W]
-        sem = lambda q: "col%d" % call[q][0]
-        for x in "cp":
-            reg = [(name + x, call[q][2], call[q][2] + call[q][1]) for q in call if q != r]
-            if x == "c":
-                send(call, sem, lambda q: mine(q, "c").bitcast(dt.uint8), lambda q: view(q, "c").bitcast(dt.uint8), reg, 1 if call is ADV else 0)
-            else:
-                send(call, sem, lambda q: mine(q, "p"), lambda q: view(q, "p"), reg, 2 if call is ADV else 0)
-
-    def own(call, name):
-        if r not in call:
-            return
-        t, W, b = call[r]
-        nm, c0 = land[t]
-        a = c0 + W * r
-        dma("y", "own%d" % t, [(T[nm + "c"][:, a:a + W].bitcast(dt.uint8), T[name + "c"][:, b:b + W].bitcast(dt.uint8),
-                                [(name + "c", b, b + W)], [(nm + "c", a, a + W)]),
-                               (T[nm + "p"][:, a:a + W], T[name + "p"][:, b:b + W], [(name + "p", b, b + W)], [(nm + "p", a, a + W)])])
-
-    def engines_in(s, who):
-        return len(_engine_sets(topo, cores, s, who, 1 if who is ADV else 0)[core])
-
-    def cc(t, s):
-        return 8 * NR * (RD - t) + 8 * (NR - 1 - s)
-
-    width, known = {}, {}
-    for t in range(1, RD + 1):
-        W, top, call = RECV[t, r]
-        width[t], known[t] = W, min(top, r - 1)
-        total["col%d" % t] = sum(2 * engines_in(s, call) for s in ALL if s != r)
-        nm, c0 = land[t]
-        for s in ALL:
-            if s != r:
-                for x in "cp":
-                    log[nm + x] = log.get(nm + x, []) + [(c0 + W * s, c0 + W * s + W, True, ("col%d" % t, total["col%d" % t]))]
-        for nm, grp, to in TELL[t]:
-            grp = [s for s in grp if s != r and r in to]
-            if grp:
-                total[nm] = sum(engines_in(s, to) for s in grp)
-            for s in grp:
-                log["cnt"] = log.get("cnt", []) + [(cc(t, s), cc(t, s) + 1, True, (nm, total[nm]))]
-    nl = {t: NR * width[t] for t in width}
-    exact = {t: known[t] == r - 1 for t in known}
-    ahead = RECV[1, r][2] is ADV
-
-    dma("y", "dx", [(T.xt[:, 0:256], T.x[:, :], [], [("xt", 0, 256)])])
-    dma("s", "dq", [(T.xt[:, 256:512], T.qx[:, 0:256], [], [("xt", 256, 512)])])
-    dma("y", "dw0", [(T.wt[:, 0:512], T.w[:, 0:512], [], [("wt", 0, 512)])])
-    dma("s", "du", [(T.us[:, 0:8], T.u[:, 0:8], [], [("us", 0, 8)])])
-    dma("s", "dw1", [(T.wt[:, 512:1024], T.w[:, 512:1024], [], [("wt", 512, 1024)])])
-    dma("y", "dw2", [(T.wt[:, 1024:1536], T.w[:, 1024:1536], [], [("wt", 1024, 1536)])])
-    dma("s", "dw3", [(T.wt[:, 1536:2048], T.w[:, 1536:2048], [], [("wt", 1536, 2048)])])
-
-    fill(rf("zt", 0, 512), 0.0)
-    quant("zq", 0, 128, "zt", 0, 512, [("zt", 0, 512)])
-
-    def pad(sem, nm, a):
-        if a < 128:
-            return dma("y", sem, [(T[nm + "c"][:, a:128].bitcast(dt.uint8), T.zqc[:, a:128].bitcast(dt.uint8), [("zqc", a, 128)],
-                                   [(nm + "c", a, 128)]),
-                                  (T[nm + "p"][:, a:128], T.zqp[:, a:128], [("zqp", a, 128)], [(nm + "p", a, 128)])])
-        return []
-    fill(rf("ut", 8, 512), 0.0)
-    lu = new("ow", 16, 2)
-    fill(sub(lu, 0, 8), 0)
-    fill(sub(lu, 8, 16), 1)
-    fill(rf("ta1", 256, 512), 0.0, ("ta1.z", 0, 1))
-    six = fl(96)
-    fill(six, 16.0)
-    quant("xq", 0, 128, "xt", 0, 512, [("xt", 0, 512)])
-    send_pair(ADV, "xq")
-    act(rf("ut", 0, 4), rf("us", 0, 4), ACT.Copy)
-    act(rf("ut", 4, 8), rf("us", 4, 8), ACT.Copy, scale=-1.0)
-    quant("uq", 0, 128, "ut", 0, 512, [("ut", 0, 512)])
-    pick("u2", 0, 256, "uq", 0, 128, lu)
-    for b in range(4):
-        quant("wq", 128 * b, 128 * b + 128, "wt", 512 * b, 512 * b + 512, [("wt", 512 * b, 512 * b + 512)])
-    CU = {t: rf("cu%d" % t, 8, 72) for t in range(1, RD + 1)}
-    CN = {t: rf("cu%d" % t, 71, 72) for t in range(1, RD + 1)}
-    fill(rf("cnt", 8 * NR * RD, 8 * NR * RD + 8), 0.0)
-    for t in range(1, RD + 1):
-        fill(rf("cu%d" % t, 0, 8), 0.0)
-    own(ADV, "xq")
-    pad("p1", "l1", nl[1])
+        quant(dst, n, "tl", 0, TL)
+        node("t", [mm("pd", 0, "u2", 0, dst, 0, n, True, False), mm("pd", 0, "u2", 128, dst, 0, n, False, True)],
+             mmr("u2", 0, dst, 0, n) + mmr("u2", 128, dst, 0, n), [("pd", 0, 512)], 0.0024 * (n + 16))
 
     def iota(out, pattern, base, ch):
-        n = 1
-        for _st, c in pattern:
-            n *= c
         if out[0] == "iw":
             f = lambda: g.iota(ap(out), pattern, base, ch)
         else:
             f = lambda: g.iota(ap(out), pattern, base, ch, allow_small_or_imprecise_dtypes=True)
-        node("g", [f], [], rg(out), 0.13 + 0.0017 * n)
+        node("g", [f], [], rg(out), 0.13 + 0.002 * cols(out))
+        return out
 
-    NC = NR * RD + 1
-    ip, i33 = new("iw", 1), fl(NC)
-    iota(ip, [[0, 1]], 0, 1)
-    iota(i33, [[1, NC]], 0, 0)
-    pl16, q4, nx = fl(64), fl(4), fl(64)
-    iota(pl16, [[0, 4], [1, 16]], 0, 0)
-    iota(q4, [[16, 4]], 0, 0)
-    iota(nx, [[1, 64]], PL * r - NR * PL, 0)
-    if ahead:
-        dstat = fl(nl[1])
-        iota(dstat, [[1, 8], [8, width[1]]], 0, 0)
-    tabs = {}
-    for t in range(1, RD + 1):
-        W = width[t]
-        if W not in tabs and not (t == 1 and ahead):
-            tabs[W] = (fl(8 * W), fl(8 * W), fl(8 * W), fl(8 * W))
-            iota(tabs[W][0], [[-1, 8], [8, W]], 0, 0)
-            iota(tabs[W][1], [[1, 8], [0, W]], 0, 0)
-    NW = {t: fl(64 + nl[t]) for t in range(1, RD + 1)}
-    WW = {t: fl(64 + nl[t]) for t in range(1, RD)}
-    jf, t8, t8w, k0, jh = fl(1), fl(1), fl(1), fl(1), fl(1)
-    i1, i2, i3 = new("iw", 1), new("iw", 1), new("iw", 1)
-    big, wm, rst, p4, hm, hw = fl(1), fl(64), fl(64), fl(4), fl(NC), fl(9)
-    ts(i1, ip, 15, None, OP.bitwise_and)
-    ts(i2, i1, 1, None, OP.logical_shift_right)
-    ts(i3, i1, 1, None, OP.bitwise_and)
-    fill(big, 1e29)
-    ts(t8w, i2, -1.0, 4.0, OP.mult, OP.add)
-    ts(k0, i3, 8.0, 3.5 - r, OP.mult, OP.add)
-    KT = {"two": k0}
+    def dst_id(q):
+        rid, pid, _s = topo.addr(cores[q])
+        return DstId(rid=rid, pnc=pid)
 
-    def table(names, first):
-        a, b, c = fl(1), fl(1), fl(1)
-        ts(a, i2, float(first), 0.0, OP.subtract, OP.max)
-        ts(b, a, 16.0, None, OP.mult)
-        tt(c, k0, b, OP.add)
-        for n in names:
-            KT[n] = c
-    table(("win", "mid"), 4)
-    ts(t8w, t8w, 0.0, None, OP.max)
-    ts(big, big, 1e9, None, OP.mult)
-    ts(jf, i1, 0.0, None, OP.add)
-    ts(hw, sub(i33, 0, 9), t8w, None, OP.not_equal)
-    ts(t8, i2, -1.0, 8.0, OP.mult, OP.add)
-    ts(wm, pl16, jf, None, OP.is_equal)
-    ts(rst, pl16, 0.5, None, OP.is_gt)
-    ts(hm, i33, t8, None, OP.not_equal)
-    ts(p4, q4, jf, None, OP.add)
-    ts(jh, jf, 0.5, None, OP.add)
-    table(("end",), 6)
-    table(("low",), 2)
-    act(sub(NW[1], 0, 64), nx, ACT.Copy, scale=0.125)
-    if ahead:
-        act(sub(NW[1], 64, 64 + nl[1]), dstat, ACT.Copy, scale=0.125)
-    for W in tabs:
-        ts(tabs[W][2], tabs[W][0], 3.5, None, OP.add)
-        act(tabs[W][3], tabs[W][1], ACT.Copy, scale=0.125)
-    LN = fl(128)
-    if nl[1] < 128:
-        fill(rf("tl1", 4 * nl[1], 512), 0.0, ("tl1.z", 0, 1))
-    fill(rf("tl2", 4 * nl[2], 512), 0.0, ("tl2.z", 0, 1))
-    fill(sub(LN, 64, 128), -64.125)
-    late += pad("p2", "l2", nl[2])
-    late += pad("p4", "a2", 64)
-    late += dma("y", "dv", [(T.vt[:, :], T.v[:, :], [], [("vt", 0, 512)])])
-    late += pad("p3", "l3", nl[3])
-    late += pad("p5", "a3", 64)
-    late += dma("y", "pg", [(T.lgc[:, 64:128].bitcast(dt.uint8), T.zqc[:, 64:128].bitcast(dt.uint8), [("zqc", 64, 128)], [("lgc", 64, 128)]),
-                            (T.lgp[:, 64:128], T.zqp[:, 64:128], [("zqp", 64, 128)], [("lgp", 64, 128)])])
-    BR, FB, NOLD, THR, LIST, KK, STW, STS, SLOT, CF, stop, LC = {}, {}, {}, {}, {}, {}, {}, {}, {}, {}, {}, {}
-    acc = [p4]
-    place = {1: "m0", 2: "a2", 3: "a3", 4: "ff"}
-    WP = {t: fl(64) for t in range(1, RD + 1)}
+    def call(tr, to, regs, after):
+        k = node("g", [lambda: g.remote_dma_fused(tr, local_sem=T.sem.sent)], regs, [], EST["issue"] + EST["transfer"] * len(tr), "sent",
+                 [x[:2] for x in to])
+        nodes[k]["on"] = [(x[0], x[2]) for x in to]
+        nodes[k]["deps"] |= set(after)
+        return k
+
+    first = {t: 64 if LAND[t, r][0] == "adv" else 0 for t in range(1, RD + 1)}
+
+    def spot(t, q, s):
+        return (64 if LAND[t, q][0] == "adv" else 0) + PL + CS + LAND[t, q][1] * ((s - q) % NR - 1)
+
+    mine = dict([(LAND[t, r][0], t) for t in range(1, RD + 1)])
+    turn = dict([(n, (LAND[mine[n], r][2] + LAND[mine[n], r][1]) % CS) for n in mine if n != "adv"])
+
+    def send(name, buf, c0):
+        who = [(t, q) for (t, q) in sorted(LAND) if LAND[t, q][0] == name and q != r]
+        last = []
+        for x in "cp":
+            eng = _engine_sets(topo, cores, r, name, x == "p" and name == "adv")
+            for W in sorted(set([LAND[k][1] for k in who])):
+                tr, to, regs = [], [], []
+                for t, q in who:
+                    if LAND[t, q][1] == W:
+                        a, b = c0 + (LAND[t, q][2] - turn.get(name, 0)) % CS, spot(t, q, r)
+                        src, dst = T[buf + x][:, a:a + W], T["a%d%s" % (t, x)][:, b:b + W]
+                        if x == "c":
+                            src, dst = src.bitcast(dt.uint8), dst.bitcast(dt.uint8)
+                        tr.append(RemoteDMATransfer(dst_ids=[dst_id(q)], dma_engine_mask=_mask(eng[q]), remote_sem=T.sem["col%d" % t], src=src,
+                                                    dst=dst))
+                        total["sent"] = total.get("sent", 0) + len(eng[q])
+                        to.append((q, "col%d" % t, eng[q]))
+                        regs.append((buf + x, a, a + W))
+                last = [call(tr, to, regs, last)]
+
+    def cc(n):
+        return 8 * (NS - 1 - n)
+
+    def slot(n):
+        return rf("cnt", cc(n), cc(n) + 1)
 
     def tell(t, src):
-        me = rf("cnt", cc(t, r), cc(t, r) + 1)
-        for nm, grp, to in TELL[t]:
-            if r in grp:
-                send(to, lambda q: nm, lambda q: ap(src), lambda q: ap(me), rg(src))
-        act(me, src, ACT.Copy)
+        sem, who, n, _f = TELL[t, r]
+        far, near, _e = _pools(topo, cores, r)
+        parts = []
+        for pool, off in ((far, True), (near, False)):
+            to = [q for q in who if q != r and _away(topo, cores, r, q) == off]
+            if to:
+                parts.append((RemoteDMATransfer(dst_ids=[dst_id(q) for q in to], dma_engine_mask=_mask(pool), remote_sem=T.sem[sem + "nf"[off]],
+                                                srcs=[ap(src)], dsts=[ap(slot(n)) for q in to]), [(q, sem + "nf"[off], pool) for q in to]))
+                total["sent"] = total.get("sent", 0) + len(pool)
+        alone = t == 1 and not any(k[0] == "adv" and not _away(topo, cores, r, q) for (_t, q), k in LAND.items())
+        for grp in ([parts[:1], parts[1:]] if alone else [parts]):
+            call([p[0] for p in grp], [d for p in grp for d in p[1]], rg(src), early if t == 1 else [])
+        if r in who:
+            act(slot(n), src, ACT.Copy)
 
-    def stops(t):
-        k = scan(CU[t], WP[t], sub(six, 0, 64), 0.0, OP.add, OP.min)
-        if t == 1:
-            for i in late:
-                nodes[i]["deps"].add(k)
-            tell(1, CN[1])
-        stop[t] = fl(64)
-        tt(stop[t], CU[t], rf("cu%d" % t, 7, 71), OP.subtract)
-        CF[t] = fl(1)
-        act(CF[t], CN[t], ACT.Copy)
+    def arrives(buf, a, b, sem):
+        log[buf] = log.get(buf, []) + [(a, b, True, (sem, total[sem]))]
 
-    def old(t):
-        to = fl(64)
-        act(to, stop[t], ACT.Copy, scale=big)
-        layer(place[t], 0, "ta1", 64, "m%d" % t, 0, (0,))
-        diff("pd0", "m%d" % t, 0)
-        w, NOLD[t] = sub(WW[t], 0, 64), fl(1)
-        tt(w, rf("pd0", 0, 64), to, OP.is_gt)
-        total_of(NOLD[t], w)
+    told = [(TELL[k][0] + "nf"[_away(topo, cores, k[1], r)], k[1], TELL[k][2]) for k in TELL if k[1] != r and r in TELL[k][1]]
+    for sem, s, n in told:
+        total[sem] = total.get(sem, 0) + len(_pools(topo, cores, s)[0 if _away(topo, cores, s, r) else 1])
+    for sem, s, n in told:
+        arrives("cnt", cc(n), cc(n) + 1, sem)
 
-    def wrap(t):
-        k, a, b = fl(64), fl(64), fl(64)
-        tt(k, stop[t], CU[t], OP.mult)
-        tt(a, k, wm, OP.mult)
-        scan(b, rst, a, 0.0, OP.mult, OP.add)
-        KK[t], STW[t] = sub(b, 15, 64, 16), fl(4)
-        act(STW[t], KK[t], ACT.Sign)
-        e, f, STS[t] = fl(4), fl(4), fl(4)
-        act(STS[t], STW[t], ACT.Copy, scale=float(width[t]))
-        act(e, STW[t], ACT.Copy, scale=64.0)
-        if exact[t]:
-            h = fl(4)
-            ts(f, KK[t], 8.5, None, OP.is_ge)
-            tt(h, e, f, OP.add)
-            e = h
-        SLOT[t] = fl(4)
-        tt(SLOT[t], e, p4, OP.max)
+    def landing(t):
+        name, W = LAND[t, r][:2]
+        total["col%d" % t] = sum(2 * len(_engine_sets(topo, cores, s, name)[r]) for s in ALL if s != r)
+        for x in "cp":
+            arrives("a%d%s" % (t, x), first[t] + PL + CS, first[t] + PL + CS + (NR - 1) * W, "col%d" % t)
 
-    def since(t, first):
-        return rf("cnt", cc(t, first), 8 * NR * RD, 8)
+    width = {t: LAND[t, r][1] for t in range(1, RD + 1)}
+    real = {t: PL + CS + (NR - 1) * width[t] for t in width}
+    late = {t: LAND[t, r][4] for t in width}
 
-    def base(t):
-        BR[t] = fl(1)
-        if r == 0 and t == 1:
-            fill(BR[t], 0.0)
-        elif r == 0:
-            total_of(BR[t], since(t - 1, NR - 1))
-        else:
-            total_of(BR[t], since(t, r - 1))
+    dma("s", "du", [(T.xt[:, 288:296], T.u[:, 0:8], [], [("xt", 288, 296)])])
+    dma("y", "dh", [(T.xt[:, 256:288], T.qx[:, 0:32], [], [("xt", 256, 288)])])
+    dma("s", "dx", [(T.xt[:, 0:256], T.x[:, :], [], [("xt", 0, 256)])])
+    for b in range(4):
+        dma("ys"[b % 2], "dw%d" % b, [(T.wt[:, 512 * b:512 * b + 512], T.w[:, 512 * b:512 * b + 512], [], [("wt", 512 * b, 512 * b + 512)])])
+    dma("y", "dq", [(T.qt[:, 0:256], T.qx[:, 0:256], [], [("qt", 0, 256)])])
 
-    def window(t):
-        if t == 1 and ahead:
-            return
-        if exact[t]:
-            FB[t] = BR[t]
-        else:
-            FB[t] = fl(1)
-            total_of(FB[t], since(t, known[t]) if known[t] >= 0 else since(t - 1, NR - 1))
-        n, W = nl[t], width[t]
-        i = new("iw", n)
-        ts(i, tabs[W][2], FB[t], 0.125, OP.add, OP.mult)
-        tt(sub(NW[t], 64, 64 + n), i, tabs[W][3], OP.add)
+    fill(rf("xt", 296, 512), 0.0)
+    fill(rf("tl", 0, 640), 0.0, TL)
+    fill(rf("qt", 256, 512), 0.0)
+    lu = new("ow", 16, 2)
+    fill(sub(lu, 0, 8), 8)
+    fill(sub(lu, 8, 16), 9)
+    act(rf("xt", 292, 296), rf("xt", 292, 296), ACT.Copy, scale=-1.0)
+    quant("xq", 128, "xt", 0, [("xt", 0, 512)])
+    send("adv", "xq", 64)
+    pick("u2", 0, 256, "xq", 64, 128, lu)
+    for b in range(4):
+        quant("wq", 128, "wt", 512 * b, [("wt", 512 * b, 512 * b + 512)], 128 * b)
+    for t in (2, 3):
+        if real[t] < 128:
+            early.append(quant("a%d" % t, 128, "tl", 0, TL))
+    quant("lg", 128, "tl", 0, TL)
 
-    def threshold(t):
-        n8, e, f, hi = sub(NW[t], 64, 64 + nl[t]), fl(1), fl(1), fl(nl[t])
-        act(f, BR[t], ACT.Copy, scale=0.125)
-        act(e, CF[t], ACT.Identity, scale=0.125, bias=f)
-        ts(hi, n8, e, big, OP.is_ge, OP.mult)
-        THR[t] = hi
-        if not exact[t]:
-            lo, THR[t] = fl(nl[t]), fl(nl[t])
-            ts(lo, n8, f, big, OP.is_lt, OP.mult)
-            tt(THR[t], lo, hi, OP.max)
+    ip, row, pl16 = iota(new("iw", 1), [[0, 1]], 0, 1), iota(fl(PL), [[1, PL]], 0, 0), iota(fl(PL), [[0, 4], [1, 16]], 0, 0)
+    six, cap = fill(fl(160), float(CS)), fill(fl(PL), OFF + CS)
+    cu = fl(72 * RD)
+    fill(sub(cu, 7, 72 * RD, 72), OFF)
+    big = fill(fl(1), 1e29)
+    ts(big, big, 1e9, None, OP.mult)
+    ji = ts(new("iw", 1), ip, 15, None, OP.bitwise_and)
+    jf = ts(fl(1), ji, 0.0, None, OP.add)
+    jh = line(jf, 1.0, OFF + 0.5)
+    wm = ts(fl(PL), pl16, jf, None, OP.is_equal)
+    rst = ts(fl(PL), pl16, 0.5, None, OP.is_gt)
+    one, two = fl(8 * RD), fl(8 * RD)
+    fill(sub(one, 0, 8 * RD, 2), -1e6)
+    act(sub(two, 1, 8 * RD, 2), iota(fl(4 * RD), [[0, RD], [16, 4]], 0, 0), ACT.Identity, bias=jf)
+    p4 = sub(two, 1, 8, 2)
+    p8 = act(fl(4), p4, ACT.Copy, scale=0.125)
+    entry, made = {}, {}
+    for name in PICKS:
+        n, n0, pairs = PICKS[name]
+        key = (pairs, turn.get(name, 0)) if pairs else (0, [k[1] for k in LAND.values() if k[0] == name][0])
+        if key not in made and pairs:
+            je = ts(new("iw", 1), iota(new("iw", 1), [[0, 1]], key[1], 1), 15, None, OP.bitwise_and) if key[1] else ji
+            mn = ts(fl(1), ts(new("iw", 1), je, 1, None, OP.logical_shift_right), float(pairs), None, OP.min)
+            made[key] = (ts(fl(25), sub(row, 0, 25), mn, float(NR - n0), OP.add, OP.not_equal),
+                         ts(fl(1), mn, -16.0, ts(fl(1), je, 8.0, 3.5 - r, OP.mult, OP.add), OP.mult, OP.add))
+        elif key not in made:
+            made[key] = act(fl(1), jf, ACT.Relu, bias=float(key[1] - CS))
+        entry[name] = made[key]
+    tabs = {}
+    for W in sorted(set(width.values())):
+        a, b = iota(fl(NR * W), [[-2, NR], [16, W]], 7 - 2 * r, 0), iota(fl(NR * W), [[1, NR], [0, W]], r, 0)
+        tabs[W] = (act(a, a, ACT.Copy, scale=0.0625), act(b, b, ACT.Copy, scale=0.125))
+    NW = {t: fl(real[t]) for t in width}
+    for t in width:
+        fill(sub(NW[t], PL, PL + CS - width[t]), 1000.0)
+    act(sub(NW[1], 0, PL), row, ACT.Identity, scale=0.125, bias=(PL * r - NR * PL) / 8)
+    LN = fl(128)
+    fill(sub(LN, 64, 128), -64.125)
 
-    def make_list(t):
-        LIST[t] = new("ow", 4, 2)
-        gi, mi = new("iw", 4), new("iw", 4)
-        ts(gi, KK[t], BR[t], -1.0, OP.add, OP.add)
-        ts(mi, gi, 7, None, OP.bitwise_and)
-        a, b = fl(4), fl(4)
-        tt(a, mi, STS[t], OP.mult)
-        slot = SLOT[t]
-        if not exact[t]:
-            di, si, w, slot = gi, new("iw", 4), fl(4), fl(4)
-            if t in FB:
-                d, di = fl(4), new("iw", 4)
-                ts(d, KK[t], FB[t], -1.0, OP.subtract, OP.add)
-                ts(di, d, BR[t], None, OP.add)
-            ts(si, di, 3, None, OP.arith_shift_right)
-            tt(w, si, STW[t], OP.mult)
-            tt(slot, w, SLOT[t], OP.add)
-        tt(b, a, slot, OP.add)
-        cp(LIST[t], b)
+    sums = {}
 
-    def merge(t):
-        e = 64 + nl[t]
-        gather(WP[t + 1], sub(WW[t], 0, e), LIST[t])
-        pick(place[t + 1], 0, 64, "m%d" % t, 0, e, LIST[t])
+    def summed(view, scale):
+        if (view, scale) not in sums:
+            sums[view, scale] = fl(1)
+            act(fl(cols(view)), view, ACT.Copy, scale=scale, acc=sums[view, scale])
+        return sums[view, scale]
 
-    def newcomers(t):
-        layer(land[t][0], land[t][1], "tl1" if t == 1 else "tl2", nl[t], "m%d" % t, 64, (0, 2))
-        diff("pd1", "m%d" % t, 64)
+    def before(n):
+        return summed(rf("cnt", cc(n - 1), 8 * NS, 8), 0.125) if n else 0.0
 
-    def count(t):
-        n = nl[t]
-        ww = sub(WW[t], 64, 64 + n)
-        tt(ww, rf("pd1", 0, n), THR[t], OP.is_gt)
-        if any(r in grp for _nm, grp, _to in TELL[t + 1]):
-            cs = rf("cs%d" % (t + 1), 0, n)
-            scan(cs, ww, sub(six, 0, n), NOLD[t], OP.add, OP.min)
-            tell(t + 1, rf(cs[0], n - 1, n))
+    def among(slots, scale=0.125):
+        c = sorted(cc(n) for n in slots)
+        if len(c) == 1 and scale == 1.0:
+            return slot(slots[0])
+        return summed(rf("cnt", c[0], c[-1] + 1, c[1] - c[0] if len(c) > 1 else 1), scale)
 
     def source(name):
-        t, top, tab, calls = PICKS[name]
-        a = NR - 1 - top
-        n = NR * t + 1 - a
-        s, o = fl(n), new("ow", 1, 2)
-        m = hw if tab == "win" else hm
-        scan(s, sub(m, a, a + n), rf("cnt", cc(t, top), 8 * NR * RD + 1, 8), 0.0, OP.mult, OP.add)
-        ts(o, sub(s, n - 1, n), KT[tab], 0.125, OP.add, OP.mult)
-        pick(name, 0, 16, "xq", 64, 128, o)
-        for call in calls:
-            send_pair(call, name)
-        for call in calls:
-            own(call, name)
+        n, n0, pairs = PICKS[name]
+        o = new("ow", 1, 2)
+        if pairs:
+            s = scan(fl(n), sub(entry[name][0], 0, n), rf("cnt", cc(n - 1), 8 * NS, 8), 0.0, OP.mult, OP.add)
+            ts(o, sub(s, n - 1, n), entry[name][1], 0.125, OP.add, OP.mult)
+        else:
+            ts(o, entry[name], before(n), (3.5 - r) / 8, OP.add, OP.add)
+        buf, c0 = ("a%d" % mine[name], PL) if name in mine else (name, 0)
+        pick(buf, c0, c0 + CS, "qq", 0, 64, o)
+        send(name, buf, c0)
+
+    WP, THR, CU, END, CF8, KK, LIST, LC = {}, {}, {}, {}, {}, {}, {}, {}
+    acc = [p4]
+
+    def count(t, ww):
+        n, more = cols(ww), TELL[t, r][3]
+        if TELL[t, r][1]:
+            init, top = 0.0, sub(six, 0, n)
+            if more:
+                init = among(more, 1.0)
+                top = act(fl(n), top, ACT.Identity, bias=init)
+            cs = scan(rf("cs%d" % t, 0, n), ww, top, init, OP.add, OP.min)
+            tell(t, sub(cs, n - 1, n))
+
+    def stops(t):
+        CU[t], END[t] = sub(cu, 72 * t - 64, 72 * t), sub(cu, 72 * t - 1, 72 * t)
+        scan(CU[t], WP[t], cap, OFF, OP.add, OP.min)
+        stop = tt(fl(PL), CU[t], sub(cu, 72 * t - 65, 72 * t - 1), OP.subtract)
+        if t < RD:
+            THR[t] = fl(real[t])
+            act(sub(THR[t], 0, PL), stop, ACT.Copy, scale=big)
+        a = tt(fl(PL), tt(fl(PL), CU[t], wm, OP.mult), stop, OP.mult)
+        KK[t] = sub(scan(fl(PL), rst, a, 0.0, OP.mult, OP.add), 15, PL, 16)
+        CF8[t] = line(END[t], 0.125, -OFF / 8)
+
+    def window(t):
+        W, X = width[t], before(LAND[t, r][3])
+        if first[t]:
+            o = ts(new("ow", 1, 2), jf, float(CS - W), 0.0, OP.subtract, OP.max)
+            pick("a1", first[t] + PL, first[t] + PL + CS, "qq", 0, 64, o)
+        i = ts(new("iw", NR * W), tabs[W][0], X, None, OP.add)
+        tt(sub(NW[t], PL + CS - W, real[t]), i, tabs[W][1], OP.add)
+
+    def wants(t):
+        X, n8, out, ww = before(LAND[t, r][3]), sub(NW[t], PL, real[t]), sub(THR[t], PL, real[t]), fl(real[t])
+        last = [n for n in late[t] for k in TELL.values() if k[2] == n and k[0][0] == "t"]
+        if late[t]:
+            h = line(END[t], 0.0625, -(OFF + 1) / 16)
+        if last:
+            d = ts(fl(cols(n8)), n8, before(last[0]), h, OP.subtract, OP.subtract)
+            act(d, d, ACT.Abs, scale=-8.0, bias=among(last, 1.0))
+            ts(out, rf("pd", PL, real[t]), 0.0, line(h, 8.0, 0.25), OP.is_gt, OP.mult)
+            tt(sub(ww, 0, PL), rf("pd", 0, PL), sub(THR[t], 0, PL), OP.is_gt)
+            tt(sub(ww, PL, real[t]), d, out, OP.is_lt)
+            return ww
+        if late[t]:
+            d = ts(fl(cols(n8)), n8, X, h, OP.subtract, OP.subtract)
+            act(d, d, ACT.Abs, scale=-1.0, bias=among(late[t]))
+            ts(out, d, h, big, OP.is_gt, OP.mult)
+        else:
+            ts(out, n8, line(CF8[t], 1.0, X) if X else CF8[t], big, OP.is_ge, OP.mult)
+        return tt(ww, rf("pd", 0, real[t]), THR[t], OP.is_gt)
+
+    def make_list(t):
+        W, X = width[t], before(LAND[t, r][3])
+        c0 = float(PL + CS - W - W * (OFF + 1 + r))
+        k8 = line(KK[t], 0.125, -(OFF + 4.5 + r) / 8)
+        if late[t]:
+            Y = among(late[t])
+            xw = line(X, 8.0 * W, c0) if X else c0
+            q = ts(new("iw", 4), k8, X, Y, OP.add, OP.add)
+            s = ts(new("iw", 4), k8, r / 8, Y, OP.add, OP.add)
+        else:
+            Y, xw = X, c0
+            q = ts(new("iw", 4), k8, X, None, OP.add)
+            s = ts(new("iw", 4), k8, r / 8, None, OP.add)
+        tt(sub(one, 8 * t - 7, 8 * t, 2), s, line(KK[t], float(W), xw), OP.add)
+        ts(sub(two, 8 * t - 8, 8 * t, 2), q, Y, -8.0 * W, OP.subtract, OP.mult)
+        both = scan(fl(8), sub(one, 8 * t - 8, 8 * t), sub(two, 8 * t - 8, 8 * t), 0.0, OP.add, OP.max)
+        LIST[t] = cp(new("ow", 4, 2), sub(both, 1, 8, 2))
 
     def take_log(t):
-        a, b = fl(63), fl(1)
-        o = new("ow", 1, 2)
-        act(a, sub(CU[t], 0, 63), ACT.Sign, scale=-1.0, bias=jh, acc=b)
+        b, o = fl(1), new("ow", 1, 2)
+        act(fl(63), sub(CU[t], 0, 63), ACT.Sign, scale=-1.0, bias=jh, acc=b)
         ts(o, b, 63.0, 0.5, OP.add, OP.mult)
-        pick("lg", 16 * t - 16, 16 * t, place[t], 0, 64, o)
-        gather(sub(LN, 16 * t - 16, 16 * t), sub(NW[t], 0, 64), o)
-        LC[t] = CF[t]
-        if t > 1:
-            LC[t] = fl(1)
-            act(LC[t], CF[t], ACT.Identity, bias=LC[t - 1])
-        m, c, d = fl(1), fl(4), fl(4)
-        ts(m, CF[t], -1.0, 16.0, OP.mult, OP.add)
-        ts(c, p4, LC[t], m, OP.is_ge, OP.mult)
-        tt(d, acc[-1], c, OP.add)
-        acc.append(d)
+        pick("lg", 16 * t - 16, 16 * t, "a%d" % t, first[t], first[t] + PL, o)
+        gather(sub(LN, 16 * t - 16, 16 * t), sub(NW[t], 0, PL), o)
+        LC[t] = line(CF8[t], 1.0, LC[t - 1]) if t > 1 else CF8[t]
+        acc.append(tt(fl(4), acc[-1], ts(fl(4), p8, LC[t], line(END[t], -1.0, OFF + CS), OP.is_ge, OP.mult), OP.add))
 
-    layer("xq", 0, "ta1", 64, "m0", 0, (0, 2))
-    diff("pd0", "m0", 0)
-    ts(WP[1], rf("pd0", 0, 64), 0.0, None, OP.is_gt)
-    stops(1)
-    source("s1")
-    for t in (1, 2, 3):
-        if t > 1:
-            merge(t - 1)
-            stops(t)
-        old(t)
-        if t == 3:
-            source("s4")
-        base(t)
+    layer("xq", 0, PL, first[1], "a1")
+    quant("qq", 128, "qt", 0, [("qt", 0, 512), ("a1c", 0, 1)])
+    for t in width:
+        landing(t)
+    WP[1] = ts(fl(PL), rf("pd", first[1], first[1] + PL), 0.0, None, OP.is_gt)
+    count(1, WP[1])
+    dma("y", "dv", [(T.vt[:, :], T.v[:, :], [("a%dc" % mine["r1"], PL + CS, PL + CS + 1)], [("vt", 0, 512)])])
+    for t in range(1, RD + 1):
+        for name in PICKS:
+            if t == max([k for k in width if TELL[k, r][2] < PICKS[name][0] and r in TELL[k, r][1]]):
+                source(name)
+        stops(t)
         window(t)
-        threshold(t)
-        newcomers(t)
-        count(t)
-        if t == 2:
-            source("s3")
-        wrap(t)
         make_list(t)
-        if t == 1:
-            source("s2")
-        else:
-            gather(sub(NW[t], 0, 64), NW[t - 1], LIST[t - 1])
-    merge(3)
-    stops(4)
-    source("s5")
-    base(4)
-    window(4)
-    wrap(4)
-    make_list(4)
-    gather(sub(NW[4], 0, 64), NW[3], LIST[3])
-
-    for t in (1, 2, 3):
         take_log(t)
-    quant("vq", 0, 128, "vt", 0, 512, [("vt", 0, 512)])
-    take_log(4)
-    lx = new("ow", 4, 2)
-    cp(lx, acc[-1])
-    pick("fin", 0, 64, "lg", 0, 128, lx)
-    nn, sid, sid2 = fl(128), fl(128), fl(128)
-    gather(sub(nn, 0, 64), LN, lx)
-    gather(sub(nn, 64, 128), NW[4], LIST[4])
-    act(sid, nn, ACT.Copy, scale=8.0)
-    ts(sid2, sid, float(NR * PL), None, OP.add)
-    dma("y", "oc1", [(T.oc[:, 0:256], T.finc[:, 0:64].bitcast(dt.uint8), [("finc", 0, 64)], [])])
-    dma("y", "osid", [(T.sid[:, :], T.f[0:1, sid2[1]:sid2[2]], rg(sid2), [])])
+        if t < RD:
+            layer("a%d" % t, first[t], real[t], 0, "m%d" % t)
+            ww = wants(t)
+            count(t + 1, ww)
+            WP[t + 1] = gather(fl(PL), ww, LIST[t])
+            pick("a%d" % (t + 1), 0, PL, "m%d" % t, 0, real[t], LIST[t])
+            gather(sub(NW[t + 1], 0, PL), NW[t], LIST[t])
 
-    pick("fin", 64, 128, "ff", 0, 64 + nl[4], LIST[4])
+    quant("vq", 128, "vt", 0, [("vt", 0, 512), ("a%dc" % mine["r2"], PL, PL + 1)])
+    lx = cp(new("ow", 4, 2), acc[-1])
+    pick("fin", 0, 64, "lg", 0, 128, lx)
+    nn = fl(128)
+    gather(sub(nn, 0, 64), LN, lx)
+    gather(sub(nn, 64, 128), NW[RD], LIST[RD])
+    sid = line(nn, 8.0, float(NR * PL))
+    dma("y", "oc1", [(T.oc[:, 0:256], T.finc[:, 0:64].bitcast(dt.uint8), [("finc", 0, 64)], [])])
+    dma("y", "osid", [(T.sid[:, :], T.f[0:1, sid[1]:sid[2]], rg(sid), [])])
+
+    pick("fin", 64, 128, "a4", 0, real[RD], LIST[RD])
     dma("y", "oc2", [(T.oc[:, 256:512], T.finc[:, 64:128].bitcast(dt.uint8), [("finc", 64, 128)], [])])
-    node("t", [mm("py", 0, "vq", 0, "fin", 0, True, True)], mmr("vq", 0, "fin", 0), [("py", 0, 512)], 0.17)
-    ys = fl(64)
-    cp(ys, rf("py", 64, 128))
+    node("t", [mm("py", 0, "vq", 0, "fin", 0, 128, True, True)], mmr("vq", 0, "fin", 0, 128), [("py", 0, 512)], 0.17)
+    ys = cp(fl(64), rf("py", 64, 128))
     dma("y", "oy", [(T.y[:, :], ap(ys), rg(ys), [])])
     dma("s", "osc", [(T.osc[4 * k:4 * k + 4, :], T.finp[32 * k:32 * k + 4, :], [("finp", 0, 128)], []) for k in range(4)])
 
@@ -651,81 +562,79 @@ def build(g, T, topo, r):
 
 def timetable(graphs, cores, topo):
     N = {(r, k): nd for r, nodes in enumerate(graphs) for k, nd in enumerate(nodes)}
-
-    def away(i, j):
-        return topo.chip(cores[i[0]]) != topo.chip(cores[j[0]])
     come = {}
     for i in N:
         for q, sem in N[i]["to"]:
             come.setdefault((q, sem), []).append(i)
-    pred, succ = {}, {i: [] for i in N}
+    succ, pred = {i: [] for i in N}, {}
     for i in N:
-        p = [((i[0], d), EST["wake"]) for d in N[i]["deps"]]
-        for sem in N[i]["ext"]:
-            p += [(j, EST["wake"] + (EST["off"] if away(i, j) else EST["on"])) for j in come[i[0], sem]]
-        pred[i] = p
-        for j, w in p:
-            succ[j].append((i, w))
+        pred[i] = [(i[0], d) for d in N[i]["deps"]] + [j for sem in N[i]["ext"] for j in come[i[0], sem]]
+        for j in pred[i]:
+            succ[j].append(i)
 
     def length(i):
         sem = N[i]["sem"]
-        return N[i]["dur"] if sem is None or sem == "sent" else LOAD.get(sem, EST["dma"])
+        return N[i]["dur"] if sem == "sent" else EST["wake"] + (LOAD.get(sem, EST["dma"]) if sem else N[i]["dur"])
 
-    rest, unmet = {}, {i: len(succ[i]) for i in N}
-    todo = [i for i in N if not unmet[i]]
-    while todo:
-        i = todo.pop()
-        rest[i] = length(i) + max([0.0] + [w + rest[j] for j, w in succ[i]])
-        for j, w in pred[i]:
-            unmet[j] -= 1
-            if not unmet[j]:
-                todo.append(j)
+    def ways(wait):
+        rest, unmet = {}, {i: len(succ[i]) for i in N}
+        todo = [i for i in N if not unmet[i]]
+        while todo:
+            i = todo.pop()
+            rest[i] = length(i) + max([0.0] + [rest[j] + wait.get(j, 0.0) + (EST["hop"] if j[0] != i[0] else 0.0) for j in succ[i]])
+            for j in pred[i]:
+                unmet[j] -= 1
+                if not unmet[j]:
+                    todo.append(j)
+        return rest
 
-    missing, at = {i: len(pred[i]) for i in N}, {i: 0.0 for i in N}
-    free, ready, lane, land, first = {}, {}, {}, {}, set()
-    order = [[] for _g in graphs]
+    def play(rest):
+        at, missing = {i: 0.0 for i in N}, {i: len(pred[i]) for i in N}
+        free, ready, lane, first, choice, wait = {}, {}, {}, set(), {}, {}
+        order = [[] for _g in graphs]
 
-    def put(i):
-        ready.setdefault((i[0], N[i]["q"]), []).append(i)
-    for i in N:
-        if not missing[i]:
-            put(i)
-    while any(ready.values()):
-        best = None
-        for k in ready:
-            if ready[k]:
-                f = free.get(k, 0.0)
-                cand = [(max(f, at[i]), -1e3 if N[i]["sem"] in LOAD else -rest[i], i) for i in ready[k]]
-                c = min(cand)
-                lim = c[0] + (EST["hold"] if k[1] == "g" else EST["look"] + EST["part"] * N[c[2]]["dur"])
-                c = min((c for c in cand if c[0] <= lim), key=lambda c: (c[1], c[2]))
-                if best is None or lim < best[0]:
-                    best = (lim, c)
-        s, _p, i = best[1]
-        nd = N[i]
-        k = (i[0], nd["q"])
-        ready[k].remove(i)
-        order[i[0]].append(i[1])
-        d = nd["dur"]
-        if nd["sem"] == "sent" and i[0] not in first:
-            first.add(i[0])
-            d += EST["first"]
-        free[k] = s + d
-        fin = s + (d if nd["sem"] == "sent" else length(i))
-        for far in (True, False):
-            n = len([q for q, _s in nd["to"] if away(i, (q, 0)) == far])
-            if n:
-                land[far] = lane[i[0], far] = max(fin + EST["fly"], lane.get((i[0], far), 0.0)) + EST["rows"] * n
-        for j, w in succ[i]:
-            f = fin + w
-            if j[0] != i[0]:
-                far = away(i, j)
-                f = land[far] + EST["wake"] + (EST["far"] if far else EST["near"])
-            at[j] = max(at[j], f)
-            missing[j] -= 1
-            if not missing[j]:
-                put(j)
-    return order
+        def put(i):
+            ready.setdefault((i[0], N[i]["q"]), []).append(i)
+            choice.pop((i[0], N[i]["q"]), None)
+
+        def choose(k):
+            f, out = free.get(k, 0.0), []
+            for c in ready[k]:
+                s = max(f, at[c])
+                e = s + N[c]["dur"] + EST["gap"]
+                end = max([s + rest[c]] + [max(at[h], e) + rest[h] for h in ready[k] if h != c])
+                out.append((LOAD.get(N[c]["sem"], 9.0), round(end / EST["grain"]), s, -rest[c], c))
+            return min(out)
+        for i in N:
+            if not missing[i]:
+                put(i)
+        while any(ready.values()):
+            for k in ready:
+                if ready[k] and k not in choice:
+                    choice[k] = choose(k)
+            k = min(choice, key=lambda k: choice[k][2:])
+            s, i = choice[k][2], choice.pop(k)[4]
+            nd = N[i]
+            ready[k].remove(i)
+            order[i[0]].append(i[1])
+            wait[i] = EST["again"] * min(s - at[i], EST["most"])
+            d = nd["dur"]
+            if nd["sem"] == "sent" and i[0] not in first:
+                first.add(i[0])
+                d += EST["first"]
+            free[k] = s + d
+            land = {}
+            for q, engines in nd.get("on", []):
+                for e in engines:
+                    lane[i[0], e] = max(s + d + EST["fly"], lane.get((i[0], e), EST["loaded"])) + EST["rows"] / len(engines)
+                land[q] = max(lane[i[0], e] for e in engines) + (EST["far"] if _away(topo, cores, i[0], q) else EST["near"])
+            for j in succ[i]:
+                at[j] = max(at[j], land[j[0]] if j[0] != i[0] else s + length(i))
+                missing[j] -= 1
+                if not missing[j]:
+                    put(j)
+        return order, wait
+    return play(ways(play(ways({}))[1]))[0]
 
 
 def rank_program(g, core, T, topo):

from concourse.bass import DstId, RemoteDMATransfer
from concourse.mybir import dt, AluOpType, AxisListType, ActivationFunctionType

OP = AluOpType
ACT = ActivationFunctionType
X4 = "float8_e4m3fn_x4"
NR, PL, CS, RD = 8, 64, 16, 4
ALL = list(range(NR))
NS = 31
TELL = {}
for _r in ALL:
    TELL[1, _r] = ("t1", ALL, _r, [])
    TELL[2, _r] = ("e1", list(range(_r + 1, 4)), 27 + _r, []) if _r < 3 else ("t2", ALL, _r + 5, [27, 28, 29] if _r == 3 else [])
    TELL[3, _r] = ("t2", ALL, _r + 13, []) if _r < 3 else ("t3", ALL, _r + 12, [30] if _r == 5 else [])
    TELL[4, _r] = ("t3", ALL, _r + 20, []) if _r < 5 else ("e4", list(range(_r + 1, NR)), _r + 20, [])
TELL[3, 3] = ("e2", ALL, 16, [])
TELL[3, 4] = ("e3", [5], 30, [])
LAND = {}
for _r in ALL:
    LAND[1, _r] = ("adv", 8, 0, 0, list(range(_r))) if _r < 3 else ("r1", 2, 2 * _r - 6, _r, [])
    LAND[2, _r] = ("r2", 2, 2 * _r - 10, _r + 5, [])
    LAND[3, _r] = ("r2", 2, 2 * _r + 6, _r + 13, [])
    LAND[4, _r] = ("r3", 2, 2 * _r, _r + 20, [])
LAND.update({(2, 0): ("r1", 6, 10, 8, []), (2, 1): ("r1", 6, 10, 8, [27]), (2, 2): ("r1", 6, 10, 8, [27, 28]),
             (2, 3): ("r1b", 10, 6, 8, [27, 28, 29]), (2, 4): ("r1b", 10, 6, 8, [8]),
             (3, 3): ("r2", 4, 12, 16, []), (3, 4): ("r2", 4, 12, 16, [16]),
             (3, 5): ("r2b", 8, 8, 16, [16, 30]), (3, 6): ("r2b", 8, 8, 16, [16, 17]), (3, 7): ("r2c", 8, 8, 17, [17, 18]),
             (4, 5): ("r3", 6, 10, 25, []), (4, 6): ("r3", 6, 10, 25, [25]), (4, 7): ("r3", 6, 10, 25, [25, 26])})
PICKS = {"r1": (8, 3, 5), "r2": (16, 2, 6), "r3": (25, 3, 5), "r1b": (8, 0, 0), "r2b": (16, 0, 0), "r2c": (17, 0, 0)}
OFF = 4000.0
LOAD = {"du": 1.8, "dh": 1.9, "dx": 2.2, "dw0": 2.7, "dw1": 3.2, "dw2": 3.7, "dw3": 4.2, "dq": 4.5}
EST = {"wake": 0.12, "gap": 0.03, "grain": 0.02, "issue": 0.15, "transfer": 0.03, "first": 1.5, "fly": 0.6, "rows": 1.2, "near": 0.7, "far": 0.8,
       "hop": 2.0, "dma": 1.8, "loaded": 4.3, "again": 0.5, "most": 0.5, "slow": 1.25}
ORDER = {}

SCRATCH = {
    "f": ("sbuf", [128, 6000], "float32"),
    "cnt": ("sbuf", [128, 8 * NS], "bfloat16"),
    "iw": ("sbuf", [128, 768], "int32"),
    "ow": ("sbuf", [128, 256], "uint16"),
    "xt": ("sbuf", [128, 512], "bfloat16"),
    "qt": ("sbuf", [128, 512], "bfloat16"),
    "wt": ("sbuf", [128, 2048], "bfloat16"),
    "vt": ("sbuf", [128, 512], "bfloat16"),
    "tl": ("sbuf", [128, 640], "bfloat16"),
    "pl": ("psum", [128, 2048], "float32"),
    "pd": ("psum", [128, 512], "float32"),
    "py": ("psum", [128, 512], "float32"),
}


def _pair(name, n):
    SCRATCH[name + "c"] = ("sbuf", [128, n], X4)
    SCRATCH[name + "p"] = ("sbuf", [128, n], "uint8")


for _k in range(1, RD + 1):
    SCRATCH["cs%d" % _k] = ("sbuf", [128, 160], "bfloat16")
    _pair("a%d" % _k, 224)
    _pair("m%d" % _k, 160)
for _n, _w in (("xq", 128), ("qq", 128), ("wq", 512), ("u2", 256), ("vq", 128), ("lg", 128), ("fin", 128), ("r1b", 16), ("r2b", 16), ("r2c", 16)):
    _pair(_n, _w)

SEMAPHORES = ["qv", "qs", "qt", "qg", "sent", "oc1", "oc2", "oy", "osid", "osc", "dv"] + list(LOAD)
SEMAPHORES += [_n + _x for _n in ("t1", "t2", "t3", "e1", "e2", "e3", "e4") for _x in "nf"]
SEMAPHORES += ["col%d" % _k for _k in range(1, RD + 1)]


def _share(cores, pool):
    k = 1
    while cores and 2 * k * len(cores) <= len(pool):
        k *= 2
    return {d: pool[i * k:i * k + k] for i, d in enumerate(cores)}


def _away(topo, cores, s, q):
    return topo.chip(cores[s]) != topo.chip(cores[q])


def _pools(topo, cores, s):
    far = topo.engines(cores[s], [cores[q] for q in ALL if _away(topo, cores, s, q)][0])
    every = topo.engines(cores[s], [cores[q] for q in ALL if q != s and not _away(topo, cores, s, q)][0])
    return far, [e for e in every if e not in far], every


def _engine_sets(topo, cores, s, name, back=False):
    far, near, every = _pools(topo, cores, s)
    who = [q for (t, q) in sorted(LAND) if LAND[t, q][0] == name and q != s]
    out, home = [q for q in who if _away(topo, cores, s, q)], [q for q in who if not _away(topo, cores, s, q)]
    if name == "adv":
        near = every
    if back:
        far, near = far[::-1], near[::-1]
    return dict(list(_share(out, far).items()) + list(_share(home, near).items()))


def _mask(engines):
    m = 0
    for e in engines:
        m |= 1 << e
    return m


def build(g, T, topo, r):
    cores = T.cores
    Q = {"v": g.vector, "s": g.scalar, "t": g.tensor, "g": g, "y": g.sync}
    nodes, log, total, early = [], {}, {}, []

    def node(q, calls, reads, writes, dur, sem=None, to=None):
        deps, ext = set(), {}
        for lst, wr in ((reads, False), (writes, True)):
            for (n, a, b) in lst:
                for (c, d, w, who) in log.get(n, []):
                    if a < d and c < b and (w or wr):
                        if isinstance(who, int):
                            deps.add(who)
                        else:
                            ext[who[0]] = who[1]
        i = len(nodes)
        nodes.append({"q": q, "calls": calls, "deps": deps, "ext": ext, "dur": dur * (1.0 if sem else EST["slow"]), "sem": sem, "to": to or []})
        for n, a, b in reads:
            log[n] = log.get(n, []) + [(a, b, False, i)]
        for n, a, b in writes:
            log[n] = [e for e in log.get(n, []) if not (a <= e[0] and e[1] <= b)] + [(a, b, True, i)]
        return i

    def dma(q, sem, items):
        total[sem] = 16 * len(items)
        ids = []
        for o, i, rd, wr in items:
            ids.append(node(q, [lambda o=o, i=i: Q[q].dma_start(o, i)], rd, wr, 0.06, sem))
        for k in ids:
            nodes[k]["batch"] = ids
        return ids

    def rf(n, a, b, st=1):
        return (n, a, b, st)

    def ap(x):
        n, a, b, st = x
        return T[n][:, a:b] if st == 1 else T[n][:, a:b:st]

    def rg(*xs):
        out = []
        for x in xs:
            if isinstance(x, tuple):
                out += [(x[0], x[1], x[2])] if x[3] == 1 else [(x[0], c, c + 1) for c in range(x[1], x[2], x[3])]
        return out

    def sv(x):
        return ap(x) if isinstance(x, tuple) else x

    def cols(x):
        return len(range(x[1], x[2], x[3]))

    pos = {"f": 0, "iw": 0, "ow": 0}

    def new(buf, n, al=8):
        a = -(-pos[buf] // al) * al
        pos[buf] = a + n
        return rf(buf, a, a + n)

    def fl(n):
        return new("f", n)

    def sub(x, a, b, st=1):
        return rf(x[0], x[1] + a, x[1] + b, st)

    def vt(n):
        return 0.04 + 0.001 * max(64, n)

    def it(n):
        return 0.06 + 0.0015 * n

    def ts(out, i, s1, s2, o0, o1=None):
        if o1 is None:
            f = lambda: g.vector.tensor_scalar(ap(out), ap(i), sv(s1), None, o0)
        else:
            f = lambda: g.vector.tensor_scalar(ap(out), ap(i), sv(s1), sv(s2), o0, o1)
        node("v", [f], rg(i, s1, s2), rg(out), vt(cols(i)))
        return out

    def tt(out, a, b, o):
        node("v", [lambda: g.vector.tensor_tensor(ap(out), ap(a), ap(b), o)], rg(a, b), rg(out), vt((1 if a[0] == "pd" else 2) * cols(a)))
        return out

    def cp(out, i):
        node("v", [lambda: g.vector.tensor_copy(ap(out), ap(i))], rg(i), rg(out), vt(cols(i)))
        return out

    def scan(out, d0, d1, init, o0, o1):
        node("v", [lambda: g.vector.tensor_tensor_scan(ap(out), ap(d0), ap(d1), sv(init), o0, o1)], rg(d0, d1, init), rg(out), vt(cols(d0)))
        return out

    def fill(x, val, tags=None):
        node("v", [lambda: g.vector.memset(ap(x), val)], [], tags or rg(x), vt(cols(x) // (1 if x[0] == "f" else 2)))
        return x

    def act(out, i, func, scale=1.0, bias=0.0, acc=None):
        kw = {}
        if acc is not None:
            kw["accum_out"] = ap(acc)
        if scale != 1.0:
            kw["scale"] = sv(scale)
        if bias != 0.0:
            kw["bias"] = sv(bias)
        node("s", [lambda: g.scalar.activation(ap(out), ap(i), func, **kw)], rg(i, scale, bias), rg(out) + (rg(acc) if acc else []), vt(cols(i)))
        return out

    def line(i, scale, bias):
        return act(fl(cols(i)), i, ACT.Identity, scale=scale, bias=bias)

    def gather(out, win, off):
        node("s", [lambda: g.scalar.activation(ap(out), ap(win).indirect(ap(off)), ACT.Copy)], rg(win, off), rg(out), it(cols(out)))
        return out

    def pick(dst, a, b, src, c, d, off):
        dc, dp, sc, sp = dst + "c", dst + "p", src + "c", src + "p"
        node("v", [lambda: g.vector.tensor_copy(T[dc][:, a:b].bitcast(dt.uint32), T[sc][:, c:d].bitcast(dt.uint32).indirect(ap(off)))],
             [(sc, c, d)] + rg(off), [(dc, a, b)], it(b - a))
        node("s", [lambda: g.scalar.activation(T[dp][:, a:b], T[sp][:, c:d].indirect(ap(off)), ACT.Copy)],
             [(sp, c, d)] + rg(off), [(dp, a, b)], it(b - a))

    def quant(dst, n, tile, c, regs, a=0):
        return node("v", [lambda: g.vector.quantize_mx(T[dst + "c"][:, a:a + n], T[dst + "p"][:, a:a + n], T[tile][:, c:c + 4 * n])], regs,
                    [(dst + "c", a, a + n), (dst + "p", a, a + n)], 0.04 + 0.001 * n)

    def mm(out, bank, st, a, mv, c, n, start, stop):
        return lambda: g.tensor.matmul_mx(T[out][:, 512 * bank:512 * bank + n], T[st + "c"][:, a:a + 128], T[st + "p"][:, a:a + 128],
                                          T[mv + "c"][:, c:c + n], T[mv + "p"][:, c:c + n], start, stop)

    def mmr(st, a, mv, c, n):
        return [(st + "c", a, a + 128), (st + "p", a, a + 128), (mv + "c", c, c + n), (mv + "p", c, c + n)]

    TL = [("tl.%d" % b, 0, 1) for b in range(4)]

    def layer(mv, c, real, at, dst):
        n = max(128, real)
        for b in range(4):
            node("t", [mm("pl", b, "wq", 128 * b, mv, c, n, True, True)], mmr("wq", 128 * b, mv, c, n), [("pl", 512 * b, 512 * b + 512)],
                 0.0012 * (n + 16))

        def relu(b):
            src, out = T.pl[:, 512 * b:512 * b + real], T.tl[:, 4 * at + b:4 * (at + real):4]
            rd = [("pl", 512 * b, 512 * b + 512)]
            if b % 2:
                node("v", [lambda: g.vector.tensor_scalar(out, src, 0.0, 0.0625, OP.max, OP.mult)], rd, [TL[b]], vt(real))
            else:
                node("s", [lambda: g.scalar.activation(out, src, ACT.Relu, scale=0.0625)], rd, [TL[b]], vt(real))
        for b in range(4):
            relu(b)
        quant(dst, n, "tl", 0, TL)
        node("t", [mm("pd", 0, "u2", 0, dst, 0, n, True, False), mm("pd", 0, "u2", 128, dst, 0, n, False, True)],
             mmr("u2", 0, dst, 0, n) + mmr("u2", 128, dst, 0, n), [("pd", 0, 512)], 0.0024 * (n + 16))

    def iota(out, pattern, base, ch):
        if out[0] == "iw":
            f = lambda: g.iota(ap(out), pattern, base, ch)
        else:
            f = lambda: g.iota(ap(out), pattern, base, ch, allow_small_or_imprecise_dtypes=True)
        node("g", [f], [], rg(out), 0.13 + 0.002 * cols(out))
        return out

    def dst_id(q):
        rid, pid, _s = topo.addr(cores[q])
        return DstId(rid=rid, pnc=pid)

    def call(tr, to, regs, after):
        k = node("g", [lambda: g.remote_dma_fused(tr, local_sem=T.sem.sent)], regs, [], EST["issue"] + EST["transfer"] * len(tr), "sent",
                 [x[:2] for x in to])
        nodes[k]["on"] = [(x[0], x[2]) for x in to]
        nodes[k]["deps"] |= set(after)
        return k

    first = {t: 64 if LAND[t, r][0] == "adv" else 0 for t in range(1, RD + 1)}

    def spot(t, q, s):
        return (64 if LAND[t, q][0] == "adv" else 0) + PL + CS + LAND[t, q][1] * ((s - q) % NR - 1)

    mine = dict([(LAND[t, r][0], t) for t in range(1, RD + 1)])
    turn = dict([(n, (LAND[mine[n], r][2] + LAND[mine[n], r][1]) % CS) for n in mine if n != "adv"])

    def send(name, buf, c0):
        who = [(t, q) for (t, q) in sorted(LAND) if LAND[t, q][0] == name and q != r]
        last = []
        for x in "cp":
            eng = _engine_sets(topo, cores, r, name, x == "p" and name == "adv")
            for W in sorted(set([LAND[k][1] for k in who])):
                tr, to, regs = [], [], []
                for t, q in who:
                    if LAND[t, q][1] == W:
                        a, b = c0 + (LAND[t, q][2] - turn.get(name, 0)) % CS, spot(t, q, r)
                        src, dst = T[buf + x][:, a:a + W], T["a%d%s" % (t, x)][:, b:b + W]
                        if x == "c":
                            src, dst = src.bitcast(dt.uint8), dst.bitcast(dt.uint8)
                        tr.append(RemoteDMATransfer(dst_ids=[dst_id(q)], dma_engine_mask=_mask(eng[q]), remote_sem=T.sem["col%d" % t], src=src,
                                                    dst=dst))
                        total["sent"] = total.get("sent", 0) + len(eng[q])
                        to.append((q, "col%d" % t, eng[q]))
                        regs.append((buf + x, a, a + W))
                last = [call(tr, to, regs, last)]

    def cc(n):
        return 8 * (NS - 1 - n)

    def slot(n):
        return rf("cnt", cc(n), cc(n) + 1)

    def tell(t, src):
        sem, who, n, _f = TELL[t, r]
        far, near, _e = _pools(topo, cores, r)
        parts = []
        for pool, off in ((far, True), (near, False)):
            to = [q for q in who if q != r and _away(topo, cores, r, q) == off]
            if to:
                parts.append((RemoteDMATransfer(dst_ids=[dst_id(q) for q in to], dma_engine_mask=_mask(pool), remote_sem=T.sem[sem + "nf"[off]],
                                                srcs=[ap(src)], dsts=[ap(slot(n)) for q in to]), [(q, sem + "nf"[off], pool) for q in to]))
                total["sent"] = total.get("sent", 0) + len(pool)
        alone = t == 1 and not any(k[0] == "adv" and not _away(topo, cores, r, q) for (_t, q), k in LAND.items())
        for grp in ([parts[:1], parts[1:]] if alone else [parts]):
            call([p[0] for p in grp], [d for p in grp for d in p[1]], rg(src), early if t == 1 else [])
        if r in who:
            act(slot(n), src, ACT.Copy)

    def arrives(buf, a, b, sem):
        log[buf] = log.get(buf, []) + [(a, b, True, (sem, total[sem]))]

    told = [(TELL[k][0] + "nf"[_away(topo, cores, k[1], r)], k[1], TELL[k][2]) for k in TELL if k[1] != r and r in TELL[k][1]]
    for sem, s, n in told:
        total[sem] = total.get(sem, 0) + len(_pools(topo, cores, s)[0 if _away(topo, cores, s, r) else 1])
    for sem, s, n in told:
        arrives("cnt", cc(n), cc(n) + 1, sem)

    def landing(t):
        name, W = LAND[t, r][:2]
        total["col%d" % t] = sum(2 * len(_engine_sets(topo, cores, s, name)[r]) for s in ALL if s != r)
        for x in "cp":
            arrives("a%d%s" % (t, x), first[t] + PL + CS, first[t] + PL + CS + (NR - 1) * W, "col%d" % t)

    width = {t: LAND[t, r][1] for t in range(1, RD + 1)}
    real = {t: PL + CS + (NR - 1) * width[t] for t in width}
    late = {t: LAND[t, r][4] for t in width}

    dma("s", "du", [(T.xt[:, 288:296], T.u[:, 0:8], [], [("xt", 288, 296)])])
    dma("y", "dh", [(T.xt[:, 256:288], T.qx[:, 0:32], [], [("xt", 256, 288)])])
    dma("s", "dx", [(T.xt[:, 0:256], T.x[:, :], [], [("xt", 0, 256)])])
    for b in range(4):
        dma("ys"[b % 2], "dw%d" % b, [(T.wt[:, 512 * b:512 * b + 512], T.w[:, 512 * b:512 * b + 512], [], [("wt", 512 * b, 512 * b + 512)])])
    dma("y", "dq", [(T.qt[:, 0:256], T.qx[:, 0:256], [], [("qt", 0, 256)])])

    fill(rf("xt", 296, 512), 0.0)
    fill(rf("tl", 0, 640), 0.0, TL)
    fill(rf("qt", 256, 512), 0.0)
    lu = new("ow", 16, 2)
    fill(sub(lu, 0, 8), 8)
    fill(sub(lu, 8, 16), 9)
    act(rf("xt", 292, 296), rf("xt", 292, 296), ACT.Copy, scale=-1.0)
    quant("xq", 128, "xt", 0, [("xt", 0, 512)])
    send("adv", "xq", 64)
    pick("u2", 0, 256, "xq", 64, 128, lu)
    for b in range(4):
        quant("wq", 128, "wt", 512 * b, [("wt", 512 * b, 512 * b + 512)], 128 * b)
    for t in (2, 3):
        if real[t] < 128:
            early.append(quant("a%d" % t, 128, "tl", 0, TL))
    quant("lg", 128, "tl", 0, TL)

    ip, row, pl16 = iota(new("iw", 1), [[0, 1]], 0, 1), iota(fl(PL), [[1, PL]], 0, 0), iota(fl(PL), [[0, 4], [1, 16]], 0, 0)
    six, cap = fill(fl(160), float(CS)), fill(fl(PL), OFF + CS)
    cu = fl(72 * RD)
    fill(sub(cu, 7, 72 * RD, 72), OFF)
    big = fill(fl(1), 1e29)
    ts(big, big, 1e9, None, OP.mult)
    ji = ts(new("iw", 1), ip, 15, None, OP.bitwise_and)
    jf = ts(fl(1), ji, 0.0, None, OP.add)
    jh = line(jf, 1.0, OFF + 0.5)
    wm = ts(fl(PL), pl16, jf, None, OP.is_equal)
    rst = ts(fl(PL), pl16, 0.5, None, OP.is_gt)
    one, two = fl(8 * RD), fl(8 * RD)
    fill(sub(one, 0, 8 * RD, 2), -1e6)
    act(sub(two, 1, 8 * RD, 2), iota(fl(4 * RD), [[0, RD], [16, 4]], 0, 0), ACT.Identity, bias=jf)
    p4 = sub(two, 1, 8, 2)
    p8 = act(fl(4), p4, ACT.Copy, scale=0.125)
    entry, made = {}, {}
    for name in PICKS:
        n, n0, pairs = PICKS[name]
        key = (pairs, turn.get(name, 0)) if pairs else (0, [k[1] for k in LAND.values() if k[0] == name][0])
        if key not in made and pairs:
            je = ts(new("iw", 1), iota(new("iw", 1), [[0, 1]], key[1], 1), 15, None, OP.bitwise_and) if key[1] else ji
            mn = ts(fl(1), ts(new("iw", 1), je, 1, None, OP.logical_shift_right), float(pairs), None, OP.min)
            made[key] = (ts(fl(25), sub(row, 0, 25), mn, float(NR - n0), OP.add, OP.not_equal),
                         ts(fl(1), mn, -16.0, ts(fl(1), je, 8.0, 3.5 - r, OP.mult, OP.add), OP.mult, OP.add))
        elif key not in made:
            made[key] = act(fl(1), jf, ACT.Relu, bias=float(key[1] - CS))
        entry[name] = made[key]
    tabs = {}
    for W in sorted(set(width.values())):
        a, b = iota(fl(NR * W), [[-2, NR], [16, W]], 7 - 2 * r, 0), iota(fl(NR * W), [[1, NR], [0, W]], r, 0)
        tabs[W] = (act(a, a, ACT.Copy, scale=0.0625), act(b, b, ACT.Copy, scale=0.125))
    NW = {t: fl(real[t]) for t in width}
    for t in width:
        fill(sub(NW[t], PL, PL + CS - width[t]), 1000.0)
    act(sub(NW[1], 0, PL), row, ACT.Identity, scale=0.125, bias=(PL * r - NR * PL) / 8)
    LN = fl(128)
    fill(sub(LN, 64, 128), -64.125)

    sums = {}

    def summed(view, scale):
        if (view, scale) not in sums:
            sums[view, scale] = fl(1)
            act(fl(cols(view)), view, ACT.Copy, scale=scale, acc=sums[view, scale])
        return sums[view, scale]

    def before(n):
        return summed(rf("cnt", cc(n - 1), 8 * NS, 8), 0.125) if n else 0.0

    def among(slots, scale=0.125):
        c = sorted(cc(n) for n in slots)
        if len(c) == 1 and scale == 1.0:
            return slot(slots[0])
        return summed(rf("cnt", c[0], c[-1] + 1, c[1] - c[0] if len(c) > 1 else 1), scale)

    def source(name):
        n, n0, pairs = PICKS[name]
        o = new("ow", 1, 2)
        if pairs:
            s = scan(fl(n), sub(entry[name][0], 0, n), rf("cnt", cc(n - 1), 8 * NS, 8), 0.0, OP.mult, OP.add)
            ts(o, sub(s, n - 1, n), entry[name][1], 0.125, OP.add, OP.mult)
        else:
            ts(o, entry[name], before(n), (3.5 - r) / 8, OP.add, OP.add)
        buf, c0 = ("a%d" % mine[name], PL) if name in mine else (name, 0)
        pick(buf, c0, c0 + CS, "qq", 0, 64, o)
        send(name, buf, c0)

    WP, THR, CU, END, CF8, KK, LIST, LC = {}, {}, {}, {}, {}, {}, {}, {}
    acc = [p4]

    def count(t, ww):
        n, more = cols(ww), TELL[t, r][3]
        if TELL[t, r][1]:
            init, top = 0.0, sub(six, 0, n)
            if more:
                init = among(more, 1.0)
                top = act(fl(n), top, ACT.Identity, bias=init)
            cs = scan(rf("cs%d" % t, 0, n), ww, top, init, OP.add, OP.min)
            tell(t, sub(cs, n - 1, n))

    def stops(t):
        CU[t], END[t] = sub(cu, 72 * t - 64, 72 * t), sub(cu, 72 * t - 1, 72 * t)
        scan(CU[t], WP[t], cap, OFF, OP.add, OP.min)
        stop = tt(fl(PL), CU[t], sub(cu, 72 * t - 65, 72 * t - 1), OP.subtract)
        if t < RD:
            THR[t] = fl(real[t])
            act(sub(THR[t], 0, PL), stop, ACT.Copy, scale=big)
        a = tt(fl(PL), tt(fl(PL), CU[t], wm, OP.mult), stop, OP.mult)
        KK[t] = sub(scan(fl(PL), rst, a, 0.0, OP.mult, OP.add), 15, PL, 16)
        CF8[t] = line(END[t], 0.125, -OFF / 8)

    def window(t):
        W, X = width[t], before(LAND[t, r][3])
        if first[t]:
            o = ts(new("ow", 1, 2), jf, float(CS - W), 0.0, OP.subtract, OP.max)
            pick("a1", first[t] + PL, first[t] + PL + CS, "qq", 0, 64, o)
        i = ts(new("iw", NR * W), tabs[W][0], X, None, OP.add)
        tt(sub(NW[t], PL + CS - W, real[t]), i, tabs[W][1], OP.add)

    def wants(t):
        X, n8, out, ww = before(LAND[t, r][3]), sub(NW[t], PL, real[t]), sub(THR[t], PL, real[t]), fl(real[t])
        last = [n for n in late[t] for k in TELL.values() if k[2] == n and k[0][0] == "t"]
        if late[t]:
            h = line(END[t], 0.0625, -(OFF + 1) / 16)
        if last:
            d = ts(fl(cols(n8)), n8, before(last[0]), h, OP.subtract, OP.subtract)
            act(d, d, ACT.Abs, scale=-8.0, bias=among(last, 1.0))
            ts(out, rf("pd", PL, real[t]), 0.0, line(h, 8.0, 0.25), OP.is_gt, OP.mult)
            tt(sub(ww, 0, PL), rf("pd", 0, PL), sub(THR[t], 0, PL), OP.is_gt)
            tt(sub(ww, PL, real[t]), d, out, OP.is_lt)
            return ww
        if late[t]:
            d = ts(fl(cols(n8)), n8, X, h, OP.subtract, OP.subtract)
            act(d, d, ACT.Abs, scale=-1.0, bias=among(late[t]))
            ts(out, d, h, big, OP.is_gt, OP.mult)
        else:
            ts(out, n8, line(CF8[t], 1.0, X) if X else CF8[t], big, OP.is_ge, OP.mult)
        return tt(ww, rf("pd", 0, real[t]), THR[t], OP.is_gt)

    def make_list(t):
        W, X = width[t], before(LAND[t, r][3])
        c0 = float(PL + CS - W - W * (OFF + 1 + r))
        k8 = line(KK[t], 0.125, -(OFF + 4.5 + r) / 8)
        if late[t]:
            Y = among(late[t])
            xw = line(X, 8.0 * W, c0) if X else c0
            q = ts(new("iw", 4), k8, X, Y, OP.add, OP.add)
            s = ts(new("iw", 4), k8, r / 8, Y, OP.add, OP.add)
        else:
            Y, xw = X, c0
            q = ts(new("iw", 4), k8, X, None, OP.add)
            s = ts(new("iw", 4), k8, r / 8, None, OP.add)
        tt(sub(one, 8 * t - 7, 8 * t, 2), s, line(KK[t], float(W), xw), OP.add)
        ts(sub(two, 8 * t - 8, 8 * t, 2), q, Y, -8.0 * W, OP.subtract, OP.mult)
        both = scan(fl(8), sub(one, 8 * t - 8, 8 * t), sub(two, 8 * t - 8, 8 * t), 0.0, OP.add, OP.max)
        LIST[t] = cp(new("ow", 4, 2), sub(both, 1, 8, 2))

    def take_log(t):
        b, o = fl(1), new("ow", 1, 2)
        act(fl(63), sub(CU[t], 0, 63), ACT.Sign, scale=-1.0, bias=jh, acc=b)
        ts(o, b, 63.0, 0.5, OP.add, OP.mult)
        pick("lg", 16 * t - 16, 16 * t, "a%d" % t, first[t], first[t] + PL, o)
        gather(sub(LN, 16 * t - 16, 16 * t), sub(NW[t], 0, PL), o)
        LC[t] = line(CF8[t], 1.0, LC[t - 1]) if t > 1 else CF8[t]
        acc.append(tt(fl(4), acc[-1], ts(fl(4), p8, LC[t], line(END[t], -1.0, OFF + CS), OP.is_ge, OP.mult), OP.add))

    layer("xq", 0, PL, first[1], "a1")
    quant("qq", 128, "qt", 0, [("qt", 0, 512), ("a1c", 0, 1)])
    for t in width:
        landing(t)
    WP[1] = ts(fl(PL), rf("pd", first[1], first[1] + PL), 0.0, None, OP.is_gt)
    count(1, WP[1])
    dma("y", "dv", [(T.vt[:, :], T.v[:, :], [("a%dc" % mine["r1"], PL + CS, PL + CS + 1)], [("vt", 0, 512)])])
    for t in range(1, RD + 1):
        for name in PICKS:
            if t == max([k for k in width if TELL[k, r][2] < PICKS[name][0] and r in TELL[k, r][1]]):
                source(name)
        stops(t)
        window(t)
        make_list(t)
        take_log(t)
        if t < RD:
            layer("a%d" % t, first[t], real[t], 0, "m%d" % t)
            ww = wants(t)
            count(t + 1, ww)
            WP[t + 1] = gather(fl(PL), ww, LIST[t])
            pick("a%d" % (t + 1), 0, PL, "m%d" % t, 0, real[t], LIST[t])
            gather(sub(NW[t + 1], 0, PL), NW[t], LIST[t])

    quant("vq", 128, "vt", 0, [("vt", 0, 512), ("a%dc" % mine["r2"], PL, PL + 1)])
    lx = cp(new("ow", 4, 2), acc[-1])
    pick("fin", 0, 64, "lg", 0, 128, lx)
    nn = fl(128)
    gather(sub(nn, 0, 64), LN, lx)
    gather(sub(nn, 64, 128), NW[RD], LIST[RD])
    sid = line(nn, 8.0, float(NR * PL))
    dma("y", "oc1", [(T.oc[:, 0:256], T.finc[:, 0:64].bitcast(dt.uint8), [("finc", 0, 64)], [])])
    dma("y", "osid", [(T.sid[:, :], T.f[0:1, sid[1]:sid[2]], rg(sid), [])])

    pick("fin", 64, 128, "a4", 0, real[RD], LIST[RD])
    dma("y", "oc2", [(T.oc[:, 256:512], T.finc[:, 64:128].bitcast(dt.uint8), [("finc", 64, 128)], [])])
    node("t", [mm("py", 0, "vq", 0, "fin", 0, 128, True, True)], mmr("vq", 0, "fin", 0, 128), [("py", 0, 512)], 0.17)
    ys = cp(fl(64), rf("py", 64, 128))
    dma("y", "oy", [(T.y[:, :], ap(ys), rg(ys), [])])
    dma("s", "osc", [(T.osc[4 * k:4 * k + 4, :], T.finp[32 * k:32 * k + 4, :], [("finp", 0, 128)], []) for k in range(4)])

    for k, nd in enumerate(nodes):
        more = set()
        for d in nd["deps"]:
            more |= set(nodes[d].get("batch", []))
        nd["deps"] = (nd["deps"] | more) - {k}
    return nodes, total, Q


def timetable(graphs, cores, topo):
    N = {(r, k): nd for r, nodes in enumerate(graphs) for k, nd in enumerate(nodes)}
    come = {}
    for i in N:
        for q, sem in N[i]["to"]:
            come.setdefault((q, sem), []).append(i)
    succ, pred = {i: [] for i in N}, {}
    for i in N:
        pred[i] = [(i[0], d) for d in N[i]["deps"]] + [j for sem in N[i]["ext"] for j in come[i[0], sem]]
        for j in pred[i]:
            succ[j].append(i)

    def length(i):
        sem = N[i]["sem"]
        return N[i]["dur"] if sem == "sent" else EST["wake"] + (LOAD.get(sem, EST["dma"]) if sem else N[i]["dur"])

    def ways(wait):
        rest, unmet = {}, {i: len(succ[i]) for i in N}
        todo = [i for i in N if not unmet[i]]
        while todo:
            i = todo.pop()
            rest[i] = length(i) + max([0.0] + [rest[j] + wait.get(j, 0.0) + (EST["hop"] if j[0] != i[0] else 0.0) for j in succ[i]])
            for j in pred[i]:
                unmet[j] -= 1
                if not unmet[j]:
                    todo.append(j)
        return rest

    def play(rest):
        at, missing = {i: 0.0 for i in N}, {i: len(pred[i]) for i in N}
        free, ready, lane, first, choice, wait = {}, {}, {}, set(), {}, {}
        order = [[] for _g in graphs]

        def put(i):
            ready.setdefault((i[0], N[i]["q"]), []).append(i)
            choice.pop((i[0], N[i]["q"]), None)

        def choose(k):
            f, out = free.get(k, 0.0), []
            for c in ready[k]:
                s = max(f, at[c])
                e = s + N[c]["dur"] + EST["gap"]
                end = max([s + rest[c]] + [max(at[h], e) + rest[h] for h in ready[k] if h != c])
                out.append((LOAD.get(N[c]["sem"], 9.0), round(end / EST["grain"]), s, -rest[c], c))
            return min(out)
        for i in N:
            if not missing[i]:
                put(i)
        while any(ready.values()):
            for k in ready:
                if ready[k] and k not in choice:
                    choice[k] = choose(k)
            k = min(choice, key=lambda k: choice[k][2:])
            s, i = choice[k][2], choice.pop(k)[4]
            nd = N[i]
            ready[k].remove(i)
            order[i[0]].append(i[1])
            wait[i] = EST["again"] * min(s - at[i], EST["most"])
            d = nd["dur"]
            if nd["sem"] == "sent" and i[0] not in first:
                first.add(i[0])
                d += EST["first"]
            free[k] = s + d
            land = {}
            for q, engines in nd.get("on", []):
                for e in engines:
                    lane[i[0], e] = max(s + d + EST["fly"], lane.get((i[0], e), EST["loaded"])) + EST["rows"] / len(engines)
                land[q] = max(lane[i[0], e] for e in engines) + (EST["far"] if _away(topo, cores, i[0], q) else EST["near"])
            for j in succ[i]:
                at[j] = max(at[j], land[j[0]] if j[0] != i[0] else s + length(i))
                missing[j] -= 1
                if not missing[j]:
                    put(j)
        return order, wait
    return play(ways(play(ways({}))[1]))[0]


def rank_program(g, core, T, topo):
    r = T.rank_of(core)
    if r is None:
        return
    if not ORDER:
        for q, o in enumerate(timetable([build(g, T, topo, q)[0] for q in ALL], T.cores, topo)):
            ORDER[q] = o
    nodes, total, Q = build(g, T, topo, r)
    value, seen = {}, {q: {} for q in Q}
    for k in ORDER[r]:
        nd = nodes[k]
        q, sem = nd["q"], nd["sem"]
        want = dict(nd["ext"])
        for d in nd["deps"]:
            want[value[d][0]] = max(want.get(value[d][0], 0), value[d][1])
        for w in want:
            if seen[q].get(w, 0) < want[w]:
                Q[q].wait_ge(T.sem[w], want[w])
                seen[q][w] = want[w]
        for c in nd["calls"][:-1]:
            c()
        if sem is None:
            total["q" + q] = total.get("q" + q, 0) + 1
            nd["calls"][-1]().then_inc(T.sem["q" + q], 1)
            value[k] = ("q" + q, total["q" + q])
        elif sem == "sent":
            nd["calls"][-1]()
            value[k] = ("sent", 0)
        else:
            nd["calls"][-1]().then_inc(T.sem[sem], 16)
            value[k] = (sem, total[sem])
    for sem in total:
        if seen["g"].get(sem, 0) < total[sem]:
            g.wait_ge(T.sem[sem], total[sem])
